import numpy as np
import ml_dtypes


def mxq(x, axis, fmt="e4m3"):
    dtype, down = {"e4m3": (ml_dtypes.float8_e4m3fn, 7), "e5m2": (ml_dtypes.float8_e5m2, 14)}[fmt]
    v = np.moveaxis(np.asarray(x, np.float32).astype(ml_dtypes.bfloat16).astype(np.float64), axis, -1)
    blocks = v.reshape(v.shape[:-1] + (-1, 32))
    amax = np.abs(blocks).max(-1, keepdims=True)
    byte = np.maximum(np.where(amax > 0, np.frexp(amax)[1] - 1 + 127, 0) - down, 1)
    scale = np.exp2(byte - 127.0)
    codes = (blocks / scale).astype(np.float32).astype(dtype).astype(np.float64)
    return np.moveaxis((codes * scale).reshape(v.shape), -1, axis)


WIDE = False


def mx_kscale(k):
    if not WIDE:
        return np.ones(k)
    levels = np.array([10, -10, 5, -5, 0])
    if k % 512:
        return np.exp2(np.random.permutation(np.resize(levels, k // 32))).repeat(32)
    a = np.empty((k // 512, 16))
    for p in range(k // 512):
        a[p, :8] = np.random.permutation(np.resize(levels, 8))
        for g in range(8):
            far = levels[np.abs(levels - a[p, g]) >= 10]
            a[p, g + 8] = far[np.random.randint(len(far))]
    return np.exp2(a.ravel()).repeat(32)


def f64(x):
    return np.asarray(x).astype(np.float64)


def striped(idx):
    return np.tile(np.asarray(idx).reshape(-1, 16).T, (8, 1)).astype(np.uint16)


def unstriped(offs):
    return offs[:16].T.reshape(-1).astype(np.int64)


B, N, T, D, DV, NQ = 1, 512, 2048, 512, 0, 256
PAGE = 32
SEG = 32


def setup_inputs():
    n = np.random.standard_normal
    pages = np.random.permutation(T // PAGE)[:B * N // PAGE]
    idx = (pages[:, None] * PAGE + np.arange(PAGE)[None, :]).reshape(-1)
    s = mx_kscale(D)[:, None]
    return {
        "qT": (n((B, D, NQ)) * s * (1.00 / np.sqrt(D))).astype(np.float32),
        "kT": (n((D, T)) / s).astype(np.float32),
        "kb": np.tile(n(T), (128, 1)).astype(np.float32),
        "offs": striped(idx),
    }


def reference(qT, kT, kb, offs):
    idx = unstriped(offs)
    pick = lambda x: x[:, idx].reshape(x.shape[0], B, N).transpose(1, 0, 2)
    a = mxq(f64(qT), 1, "e4m3").transpose(0, 2, 1) @ mxq(pick(f64(kT)), 1, "e4m3")
    a = a + pick(f64(kb))[:, :1, :]
    return a.reshape(B, NQ, N // SEG, SEG).max(-1)

@@ -1,0 +1,125 @@
+from contextlib import ExitStack
+
+import concourse.mybir as mybir
+from concourse.masks import make_identity
+
+D, T, N, NQ, PAGE = 512, 2048, 512, 256, 32
+P = 128
+PACK = 4
+CHUNK = 128
+CHUNKS = N // CHUNK
+
+F32 = mybir.dt.float32
+BF16 = mybir.dt.bfloat16
+U32 = mybir.dt.uint32
+U16 = mybir.dt.uint16
+U8 = mybir.dt.uint8
+FP8X4 = mybir.dt.float8_e4m3fn_x4
+IDENTITY = mybir.ActivationFunctionType.Identity
+
+FLOPS = 2 * NQ * N * D
+BYTES = 4 * (D * NQ + D * T + T + NQ * N // PAGE) + 2 * P * N // 16
+
+
+def tile_attend_maxsim_kb_kernel(tc, qT, kT, kb, offs, out):
+    nc = tc.nc
+    with ExitStack() as ctx:
+        held = ctx.enter_context(tc.tile_pool(name="held", bufs=1))
+        psum = ctx.enter_context(tc.psum_pool(name="psum", bufs=1))
+
+        offsets = held.tile([P, N // 16], U16, name="offsets")
+        nc.sync.dma_start(offsets[:], offs)
+
+        kb_row = held.tile([P, T], F32, name="kb_row")
+        nc.vector.memset(kb_row[:], 0.0)
+
+        kT_planes = kT.rearrange("(p t) n -> p t n", t=PACK)
+        planes = []
+        for t in range(PACK):
+            plane = held.tile([P, T], F32, name="plane%d" % t)
+            planes.append(plane)
+        q_raw = held.tile([P, PACK, NQ], F32, name="q_raw")
+        nc.sync.dma_start(planes[0][:], kT_planes[:, 0, :])
+        nc.sync.dma_start(kb_row[0:1, :], kb[0:1, :])
+        nc.sync.dma_start(planes[1][:], kT_planes[:, 1, :])
+        nc.sync.dma_start(q_raw[:], qT[0].rearrange("(p t) q -> p t q", t=PACK))
+        for t in range(2, PACK):
+            nc.sync.dma_start(planes[t][:], kT_planes[:, t, :])
+
+        identity = held.tile([P, P], F32, name="identity")
+        make_identity(nc, identity[:])
+
+        kb_listed = held.tile([P, N], F32, name="kb_listed")
+        nc.vector.tensor_copy(kb_listed[:], kb_row[:].indirect(offsets[:]))
+        kb_turned = psum.tile([P, CHUNKS, P], F32, name="turned0")
+        for s in range(CHUNKS):
+            nc.tensor.transpose(kb_turned[:, s, :], kb_listed[:, s * CHUNK : (s + 1) * CHUNK], identity[:])
+        bias = held.tile([P, CHUNKS], F32, name="bias")
+        nc.scalar.copy(bias[:], kb_turned[:, :, 0])
+
+        keys = held.tile([P, N, PACK], BF16, name="keys", align_bytes=64)
+        queries = held.tile([P, NQ, PACK], BF16, name="queries", align_bytes=64)
+        q_codes = held.tile([P, NQ], U32, name="q_codes", align_bytes=64)
+        q_scales = held.tile([P, NQ], U8, name="q_scales", align_bytes=64)
+        nc.scalar.copy(queries[:], q_raw[:].rearrange("p t q -> p q t"))
+        for t in range(PACK - 1):
+            nc.vector.tensor_copy(keys[:, :, t], planes[t][:].indirect(offsets[:]))
+            if t == 1:
+                nc.vector.quantize_mx(out=q_codes[:].bitcast(FP8X4), scales=q_scales[:], in_=queries[:].rearrange("p q t -> p (q t)"))
+
+        warm = psum.tile([P, 4, P], F32, name="turned3")
+        for t, count in ((2, 12), (3, 8)):
+            for i in range(count):
+                nc.tensor.transpose(warm[:, i % 4, :], planes[t][:, i * P % T : i * P % T + P], identity[:])
+        best = held.tile([P, NQ // P, N // PAGE], F32, name="best")
+        HALF = N // 2
+        t = PACK - 1
+        codes, scales, scores, biased, turned = [], [], [], [], []
+        for h in range(2):
+            cols = slice(h * HALF, (h + 1) * HALF)
+            code = held.tile([P, HALF], U32, name="k_codes%d" % h, align_bytes=64)
+            scale = held.tile([P, HALF], U8, name="k_scales%d" % h, align_bytes=64)
+            nc.vector.tensor_copy(keys[:, cols, t], planes[t][:].indirect(offsets[:, h * HALF // 16 : (h + 1) * HALF // 16]))
+            for c in range(2):
+                kc = slice(c * CHUNK, (c + 1) * CHUNK)
+                at = h * HALF + c * CHUNK
+                nc.vector.quantize_mx(out=code[:, kc].bitcast(FP8X4), scales=scale[:, kc], in_=keys[:, at : at + CHUNK, :].rearrange("p n t -> p (n t)"))
+            codes.append(code)
+            scales.append(scale)
+        per = CHUNK // PAGE
+
+        def score_chunk(s):
+            kc = slice(s % 2 * CHUNK, (s % 2 + 1) * CHUNK)
+            score = psum.tile([P, NQ], F32, name="scores%d" % s)
+            nc.tensor.matmul_mx(
+                out=score[:],
+                lhsT=codes[s // 2][:, kc].bitcast(FP8X4),
+                lhsT_scale=scales[s // 2][:, kc],
+                rhs=q_codes[:].bitcast(FP8X4),
+                rhs_scale=q_scales[:],
+                start=True,
+                stop=True,
+            )
+            bia = held.tile([P, NQ], F32, name="biased%d" % s)
+            nc.scalar.activation(bia[:], score[:], IDENTITY, bias=bias[:, s : s + 1])
+            biased.append(bia)
+
+        def best_of_chunk(s):
+            turn = psum.tile([P, NQ // P, CHUNK], F32, name="turned%d" % s)
+            for r in range(NQ // P):
+                nc.tensor.transpose(turn[:, r, :], biased[s][:, r * P : (r + 1) * P], identity[:])
+            nc.vector.reduce_max(
+                best[:, :, s * per : (s + 1) * per],
+                turn[:].rearrange("p r (j i) -> p r j i", i=PAGE),
+                axis=mybir.AxisListType.X,
+            )
+
+        score_chunk(0)
+        score_chunk(1)
+        best_of_chunk(0)
+        score_chunk(2)
+        best_of_chunk(1)
+        score_chunk(3)
+        best_of_chunk(2)
+        best_of_chunk(3)
+        nc.sync.dma_start(out[0].rearrange("(r p) j -> p r j", p=P), best[:])

@@ -67,10 +67,6 @@ def tile_attend_maxsim_kb_kernel(tc, qT, kT, kb, offs, out):
             if t == 1:
                 nc.vector.quantize_mx(out=q_codes[:].bitcast(FP8X4), scales=q_scales[:], in_=queries[:].rearrange("p q t -> p (q t)"))
 
-        warm = psum.tile([P, 4, P], F32, name="turned3")
-        for t, count in ((2, 12), (3, 8)):
-            for i in range(count):
-                nc.tensor.transpose(warm[:, i % 4, :], planes[t][:, i * P % T : i * P % T + P], identity[:])
         best = held.tile([P, NQ // P, N // PAGE], F32, name="best")
         HALF = N // 2
         t = PACK - 1

@@ -8,6 +8,11 @@ P = 128
 PACK = 4
 CHUNK = 128
 CHUNKS = N // CHUNK
+HALF = N // 2
+ROWS = NQ // P
+PER = CHUNK // PAGE
+CUTS = [0, 1024, 1536, 1792, 2048]
+DIRECT = [0, 3]
 
 F32 = mybir.dt.float32
 BF16 = mybir.dt.bfloat16
@@ -15,7 +20,9 @@ U32 = mybir.dt.uint32
 U16 = mybir.dt.uint16
 U8 = mybir.dt.uint8
 FP8X4 = mybir.dt.float8_e4m3fn_x4
+COPY = mybir.ActivationFunctionType.Copy
 IDENTITY = mybir.ActivationFunctionType.Identity
+ADD = mybir.AluOpType.add
 
 FLOPS = 2 * NQ * N * D
 BYTES = 4 * (D * NQ + D * T + T + NQ * N // PAGE) + 2 * P * N // 16
@@ -28,94 +35,114 @@ def tile_attend_maxsim_kb_kernel(tc, qT, kT, kb, offs, out):
         psum = ctx.enter_context(tc.psum_pool(name="psum", bufs=1))
 
         offsets = held.tile([P, N // 16], U16, name="offsets")
-        nc.sync.dma_start(offsets[:], offs)
-
         kb_row = held.tile([P, T], F32, name="kb_row")
         nc.vector.memset(kb_row[:], 0.0)
 
         kT_planes = kT.rearrange("(p t) n -> p t n", t=PACK)
-        planes = []
-        for t in range(PACK):
-            plane = held.tile([P, T], F32, name="plane%d" % t)
-            planes.append(plane)
+        planes = [held.tile([P, T], F32, name="plane%d" % t) for t in range(PACK)]
         q_raw = held.tile([P, PACK, NQ], F32, name="q_raw")
         nc.sync.dma_start(planes[0][:], kT_planes[:, 0, :])
+        nc.sync.dma_start(offsets[:], offs)
+        nc.sync.dma_start(q_raw[:], qT[0].rearrange("(p t) q -> p t q", t=PACK))
         nc.sync.dma_start(kb_row[0:1, :], kb[0:1, :])
         nc.sync.dma_start(planes[1][:], kT_planes[:, 1, :])
-        nc.sync.dma_start(q_raw[:], qT[0].rearrange("(p t) q -> p t q", t=PACK))
-        for t in range(2, PACK):
-            nc.sync.dma_start(planes[t][:], kT_planes[:, t, :])
+        nc.sync.dma_start(planes[2][:], kT_planes[:, 2, :])
+        pieces = [slice(a, b) for a, b in zip(CUTS, CUTS[1:])]
+        for piece in pieces:
+            nc.sync.dma_start(planes[3][:, piece], kT_planes[:, 3, piece])
 
         identity = held.tile([P, P], F32, name="identity")
         make_identity(nc, identity[:])
-
-        kb_listed = held.tile([P, N], F32, name="kb_listed")
-        nc.vector.tensor_copy(kb_listed[:], kb_row[:].indirect(offsets[:]))
-        kb_turned = psum.tile([P, CHUNKS, P], F32, name="turned0")
-        for s in range(CHUNKS):
-            nc.tensor.transpose(kb_turned[:, s, :], kb_listed[:, s * CHUNK : (s + 1) * CHUNK], identity[:])
-        bias = held.tile([P, CHUNKS], F32, name="bias")
-        nc.scalar.copy(bias[:], kb_turned[:, :, 0])
 
         keys = held.tile([P, N, PACK], BF16, name="keys", align_bytes=64)
         queries = held.tile([P, NQ, PACK], BF16, name="queries", align_bytes=64)
         q_codes = held.tile([P, NQ], U32, name="q_codes", align_bytes=64)
         q_scales = held.tile([P, NQ], U8, name="q_scales", align_bytes=64)
+        kb_listed = held.tile([P, N], F32, name="kb_listed")
         nc.scalar.copy(queries[:], q_raw[:].rearrange("p t q -> p q t"))
-        for t in range(PACK - 1):
+        nc.vector.tensor_copy(keys[:, :, 0], planes[0][:].indirect(offsets[:]))
+        nc.vector.tensor_copy(kb_listed[:], kb_row[:].indirect(offsets[:]))
+        kb_turned = psum.tile([P, CHUNKS, P], F32, name="bank4")
+        for s in range(CHUNKS):
+            nc.tensor.transpose(kb_turned[:, s, :], kb_listed[:, s * CHUNK : (s + 1) * CHUNK], identity[:])
+        bias = held.tile([P, CHUNKS], F32, name="bias")
+        nc.scalar.copy(bias[:], kb_turned[:, :, 0])
+        spread = psum.tile([P, len(DIRECT), P], F32, name="bank5")
+        for i, s in enumerate(DIRECT):
+            nc.tensor.transpose(spread[:, i, :], bias[:, s : s + 1].to_broadcast([P, P]), identity[:])
+        bias_rows = held.tile([P, len(DIRECT), ROWS, CHUNK], F32, name="bias_rows")
+        for r in range(ROWS):
+            nc.scalar.copy(bias_rows[:, :, r, :], spread[:])
+
+        nc.vector.quantize_mx(out=q_codes[:].bitcast(FP8X4), scales=q_scales[:], in_=queries[:].rearrange("p q t -> p (q t)"))
+        for t in (1, 2):
             nc.vector.tensor_copy(keys[:, :, t], planes[t][:].indirect(offsets[:]))
-            if t == 1:
-                nc.vector.quantize_mx(out=q_codes[:].bitcast(FP8X4), scales=q_scales[:], in_=queries[:].rearrange("p q t -> p (q t)"))
 
-        best = held.tile([P, NQ // P, N // PAGE], F32, name="best")
-        HALF = N // 2
-        t = PACK - 1
-        codes, scales, scores, biased, turned = [], [], [], [], []
-        for h in range(2):
-            cols = slice(h * HALF, (h + 1) * HALF)
-            code = held.tile([P, HALF], U32, name="k_codes%d" % h, align_bytes=64)
-            scale = held.tile([P, HALF], U8, name="k_scales%d" % h, align_bytes=64)
-            nc.vector.tensor_copy(keys[:, cols, t], planes[t][:].indirect(offsets[:, h * HALF // 16 : (h + 1) * HALF // 16]))
-            for c in range(2):
-                kc = slice(c * CHUNK, (c + 1) * CHUNK)
-                at = h * HALF + c * CHUNK
-                nc.vector.quantize_mx(out=code[:, kc].bitcast(FP8X4), scales=scale[:, kc], in_=keys[:, at : at + CHUNK, :].rearrange("p n t -> p (n t)"))
-            codes.append(code)
-            scales.append(scale)
-        per = CHUNK // PAGE
+        rounded = held.tile([P, T], BF16, name="rounded")
+        for i, piece in enumerate(pieces):
+            if i in (1, 2):
+                nc.vector.tensor_copy(rounded[:, piece], planes[3][:, piece])
+            else:
+                nc.scalar.copy(rounded[:, piece], planes[3][:, piece])
 
-        def score_chunk(s):
-            kc = slice(s % 2 * CHUNK, (s % 2 + 1) * CHUNK)
-            score = psum.tile([P, NQ], F32, name="scores%d" % s)
-            nc.tensor.matmul_mx(
-                out=score[:],
-                lhsT=codes[s // 2][:, kc].bitcast(FP8X4),
-                lhsT_scale=scales[s // 2][:, kc],
-                rhs=q_codes[:].bitcast(FP8X4),
-                rhs_scale=q_scales[:],
-                start=True,
-                stop=True,
-            )
-            bia = held.tile([P, NQ], F32, name="biased%d" % s)
-            nc.scalar.activation(bia[:], score[:], IDENTITY, bias=bias[:, s : s + 1])
-            biased.append(bia)
+        best = held.tile([P, ROWS, N // PAGE], F32, name="best")
+        codes = [held.tile([P, CHUNK], U32, name="k_codes%d" % s, align_bytes=64) for s in range(CHUNKS)]
+        scales = [held.tile([P, CHUNK], U8, name="k_scales%d" % s, align_bytes=64) for s in range(CHUNKS)]
+        scores = [psum.tile([P, ROWS, P], F32, name="bank%d" % s) for s in range(CHUNKS)]
+        biased = [held.tile([P, ROWS, P], F32, name="biased%d" % s) for s in range(CHUNKS)]
+        turned = {}
 
-        def best_of_chunk(s):
-            turn = psum.tile([P, NQ // P, CHUNK], F32, name="turned%d" % s)
-            for r in range(NQ // P):
-                nc.tensor.transpose(turn[:, r, :], biased[s][:, r * P : (r + 1) * P], identity[:])
-            nc.vector.reduce_max(
-                best[:, :, s * per : (s + 1) * per],
-                turn[:].rearrange("p r (j i) -> p r j i", i=PAGE),
-                axis=mybir.AxisListType.X,
-            )
+        def gather(h):
+            listed = offsets[:, h * HALF // 16 : (h + 1) * HALF // 16]
+            if h == 0:
+                nc.vector.tensor_copy(keys[:, :HALF, 3], planes[3][:].indirect(listed))
+            else:
+                nc.scalar.activation(keys[:, HALF:, 3], rounded[:].indirect(listed), COPY)
 
-        score_chunk(0)
-        score_chunk(1)
-        best_of_chunk(0)
-        score_chunk(2)
-        best_of_chunk(1)
-        score_chunk(3)
-        best_of_chunk(2)
-        best_of_chunk(3)
+        def quantise(s):
+            nc.vector.quantize_mx(out=codes[s][:].bitcast(FP8X4), scales=scales[s][:], in_=keys[:, s * CHUNK : (s + 1) * CHUNK, :].rearrange("p n t -> p (n t)"))
+
+        def multiply(s):
+            if s in DIRECT:
+                for r in range(ROWS):
+                    rows = slice(r * P, (r + 1) * P)
+                    nc.tensor.matmul_mx(out=scores[s][:, r, :], lhsT=q_codes[:, rows].bitcast(FP8X4), lhsT_scale=q_scales[:, rows], rhs=codes[s][:].bitcast(FP8X4), rhs_scale=scales[s][:], start=True, stop=True)
+            else:
+                nc.tensor.matmul_mx(out=scores[s][:].rearrange("p r q -> p (r q)"), lhsT=codes[s][:].bitcast(FP8X4), lhsT_scale=scales[s][:], rhs=q_codes[:].bitcast(FP8X4), rhs_scale=q_scales[:], start=True, stop=True)
+
+        def add_bias(s):
+            if s in DIRECT:
+                nc.vector.tensor_tensor(biased[s][:], scores[s][:], bias_rows[:, DIRECT.index(s), :, :], ADD)
+            else:
+                nc.scalar.activation(biased[s][:], scores[s][:], IDENTITY, bias=bias[:, s : s + 1])
+
+        def turn(s, bank):
+            turned[s] = psum.tile([P, ROWS, CHUNK], F32, name="bank%d" % bank)
+            for r in range(ROWS):
+                nc.tensor.transpose(turned[s][:, r, :], biased[s][:, r, :], identity[:])
+
+        def largest(s):
+            source = biased[s] if s in DIRECT else turned[s]
+            nc.vector.reduce_max(best[:, :, s * PER : (s + 1) * PER], source[:].rearrange("p r (j i) -> p r j i", i=PAGE), axis=mybir.AxisListType.X)
+
+        gather(0)
+        gather(1)
+        quantise(0)
+        quantise(1)
+        quantise(2)
+        quantise(3)
+        multiply(0)
+        multiply(1)
+        add_bias(0)
+        add_bias(1)
+        multiply(2)
+        add_bias(2)
+        multiply(3)
+        turn(1, 4)
+        turn(2, 5)
+        largest(0)
+        add_bias(3)
+        largest(1)
+        largest(3)
+        largest(2)
         nc.sync.dma_start(out[0].rearrange("(r p) j -> p r j", p=P), best[:])

@@ -11,7 +11,6 @@ CHUNKS = N // CHUNK
 HALF = N // 2
 ROWS = NQ // P
 PER = CHUNK // PAGE
-CUTS = [0, 1024, 1536, 1792, 2048]
 DIRECT = [0, 3]
 
 F32 = mybir.dt.float32
@@ -20,7 +19,6 @@ U32 = mybir.dt.uint32
 U16 = mybir.dt.uint16
 U8 = mybir.dt.uint8
 FP8X4 = mybir.dt.float8_e4m3fn_x4
-COPY = mybir.ActivationFunctionType.Copy
 IDENTITY = mybir.ActivationFunctionType.Identity
 ADD = mybir.AluOpType.add
 
@@ -46,10 +44,8 @@ def tile_attend_maxsim_kb_kernel(tc, qT, kT, kb, offs, out):
         nc.sync.dma_start(q_raw[:], qT[0].rearrange("(p t) q -> p t q", t=PACK))
         nc.sync.dma_start(kb_row[0:1, :], kb[0:1, :])
         nc.sync.dma_start(planes[1][:], kT_planes[:, 1, :])
-        nc.sync.dma_start(planes[2][:], kT_planes[:, 2, :])
-        pieces = [slice(a, b) for a, b in zip(CUTS, CUTS[1:])]
-        for piece in pieces:
-            nc.sync.dma_start(planes[3][:, piece], kT_planes[:, 3, piece])
+        for t in range(2, PACK):
+            nc.sync.dma_start(planes[t][:], kT_planes[:, t, :])
 
         identity = held.tile([P, P], F32, name="identity")
         make_identity(nc, identity[:])
@@ -78,13 +74,6 @@ def tile_attend_maxsim_kb_kernel(tc, qT, kT, kb, offs, out):
         for t in (1, 2):
             nc.vector.tensor_copy(keys[:, :, t], planes[t][:].indirect(offsets[:]))
 
-        rounded = held.tile([P, T], BF16, name="rounded")
-        for i, piece in enumerate(pieces):
-            if i in (1, 2):
-                nc.vector.tensor_copy(rounded[:, piece], planes[3][:, piece])
-            else:
-                nc.scalar.copy(rounded[:, piece], planes[3][:, piece])
-
         best = held.tile([P, ROWS, N // PAGE], F32, name="best")
         codes = [held.tile([P, CHUNK], U32, name="k_codes%d" % s, align_bytes=64) for s in range(CHUNKS)]
         scales = [held.tile([P, CHUNK], U8, name="k_scales%d" % s, align_bytes=64) for s in range(CHUNKS)]
@@ -93,11 +82,7 @@ def tile_attend_maxsim_kb_kernel(tc, qT, kT, kb, offs, out):
         turned = {}
 
         def gather(h):
-            listed = offsets[:, h * HALF // 16 : (h + 1) * HALF // 16]
-            if h == 0:
-                nc.vector.tensor_copy(keys[:, :HALF, 3], planes[3][:].indirect(listed))
-            else:
-                nc.scalar.activation(keys[:, HALF:, 3], rounded[:].indirect(listed), COPY)
+            nc.vector.tensor_copy(keys[:, h * HALF : (h + 1) * HALF, 3], planes[3][:].indirect(offsets[:, h * HALF // 16 : (h + 1) * HALF // 16]))
 
         def quantise(s):
             nc.vector.quantize_mx(out=codes[s][:].bitcast(FP8X4), scales=scales[s][:], in_=keys[:, s * CHUNK : (s + 1) * CHUNK, :].rearrange("p n t -> p (n t)"))

@@ -10,8 +10,6 @@ CHUNK = 128
 CHUNKS = N // CHUNK
 HALF = N // 2
 ROWS = NQ // P
-PER = CHUNK // PAGE
-DIRECT = [0, 3]
 
 F32 = mybir.dt.float32
 BF16 = mybir.dt.bfloat16
@@ -34,100 +32,113 @@ def tile_attend_maxsim_kb_kernel(tc, qT, kT, kb, offs, out):
 
         offsets = held.tile([P, N // 16], U16, name="offsets")
         kb_row = held.tile([P, T], F32, name="kb_row")
-        nc.vector.memset(kb_row[:], 0.0)
+        nc.gpsimd.memset(kb_row[:, : T // 2], 0.0)
+        nc.vector.memset(kb_row[:, T // 2 :], 0.0)
 
         kT_planes = kT.rearrange("(p t) n -> p t n", t=PACK)
         planes = [held.tile([P, T], F32, name="plane%d" % t) for t in range(PACK)]
         q_raw = held.tile([P, PACK, NQ], F32, name="q_raw")
         nc.sync.dma_start(planes[0][:], kT_planes[:, 0, :])
         nc.sync.dma_start(offsets[:], offs)
-        nc.sync.dma_start(q_raw[:], qT[0].rearrange("(p t) q -> p t q", t=PACK))
         nc.sync.dma_start(kb_row[0:1, :], kb[0:1, :])
-        nc.sync.dma_start(planes[1][:], kT_planes[:, 1, :])
-        for t in range(2, PACK):
+        for t in range(1, PACK):
             nc.sync.dma_start(planes[t][:], kT_planes[:, t, :])
+        nc.sync.dma_start(q_raw[:], qT[0].rearrange("(p t) q -> p t q", t=PACK))
 
         identity = held.tile([P, P], F32, name="identity")
         make_identity(nc, identity[:])
 
         keys = held.tile([P, N, PACK], BF16, name="keys", align_bytes=64)
-        queries = held.tile([P, NQ, PACK], BF16, name="queries", align_bytes=64)
-        q_codes = held.tile([P, NQ], U32, name="q_codes", align_bytes=64)
-        q_scales = held.tile([P, NQ], U8, name="q_scales", align_bytes=64)
         kb_listed = held.tile([P, N], F32, name="kb_listed")
-        nc.scalar.copy(queries[:], q_raw[:].rearrange("p t q -> p q t"))
         nc.vector.tensor_copy(keys[:, :, 0], planes[0][:].indirect(offsets[:]))
         nc.vector.tensor_copy(kb_listed[:], kb_row[:].indirect(offsets[:]))
-        kb_turned = psum.tile([P, CHUNKS, P], F32, name="bank4")
+        for t in (1, 2):
+            nc.vector.tensor_copy(keys[:, :, t], planes[t][:].indirect(offsets[:]))
+        kb_turned = psum.tile([P, CHUNKS, P], F32, name="bank6")
         for s in range(CHUNKS):
             nc.tensor.transpose(kb_turned[:, s, :], kb_listed[:, s * CHUNK : (s + 1) * CHUNK], identity[:])
         bias = held.tile([P, CHUNKS], F32, name="bias")
         nc.scalar.copy(bias[:], kb_turned[:, :, 0])
-        spread = psum.tile([P, len(DIRECT), P], F32, name="bank5")
-        for i, s in enumerate(DIRECT):
-            nc.tensor.transpose(spread[:, i, :], bias[:, s : s + 1].to_broadcast([P, P]), identity[:])
-        bias_rows = held.tile([P, len(DIRECT), ROWS, CHUNK], F32, name="bias_rows")
-        for r in range(ROWS):
-            nc.scalar.copy(bias_rows[:, :, r, :], spread[:])
-
-        nc.vector.quantize_mx(out=q_codes[:].bitcast(FP8X4), scales=q_scales[:], in_=queries[:].rearrange("p q t -> p (q t)"))
-        for t in (1, 2):
-            nc.vector.tensor_copy(keys[:, :, t], planes[t][:].indirect(offsets[:]))
+        spread = psum.tile([P, CHUNKS, P], F32, name="bank7")
+        for s in range(CHUNKS):
+            nc.tensor.transpose(spread[:, s, :], bias[:, s : s + 1].to_broadcast([P, P]), identity[:])
+        bias_row = held.tile([P, N], F32, name="bias_row")
+        nc.scalar.copy(bias_row[:], spread[:].rearrange("p s n -> p (s n)"))
 
         best = held.tile([P, ROWS, N // PAGE], F32, name="best")
-        codes = [held.tile([P, CHUNK], U32, name="k_codes%d" % s, align_bytes=64) for s in range(CHUNKS)]
-        scales = [held.tile([P, CHUNK], U8, name="k_scales%d" % s, align_bytes=64) for s in range(CHUNKS)]
-        scores = [psum.tile([P, ROWS, P], F32, name="bank%d" % s) for s in range(CHUNKS)]
-        biased = [held.tile([P, ROWS, P], F32, name="biased%d" % s) for s in range(CHUNKS)]
-        turned = {}
+        queries = [held.tile([P, P, PACK], BF16, name="queries%d" % r, align_bytes=64) for r in range(ROWS)]
+        q_codes = [held.tile([P, P], U32, name="q_codes%d" % r, align_bytes=64) for r in range(ROWS)]
+        q_scales = [held.tile([P, P], U8, name="q_scales%d" % r, align_bytes=64) for r in range(ROWS)]
+        k_codes = held.tile([P, N], U32, name="k_codes", align_bytes=64)
+        k_scales = held.tile([P, N], U8, name="k_scales", align_bytes=64)
+        biased = held.tile([P, ROWS, N], F32, name="biased")
+        banks = {}
 
-        def gather(h):
-            nc.vector.tensor_copy(keys[:, h * HALF : (h + 1) * HALF, 3], planes[3][:].indirect(offsets[:, h * HALF // 16 : (h + 1) * HALF // 16]))
+        def span(first, count):
+            return slice(first * CHUNK, (first + count) * CHUNK)
 
-        def quantise(s):
-            nc.vector.quantize_mx(out=codes[s][:].bitcast(FP8X4), scales=scales[s][:], in_=keys[:, s * CHUNK : (s + 1) * CHUNK, :].rearrange("p n t -> p (n t)"))
+        def weave(r):
+            nc.scalar.copy(queries[r][:], q_raw[:, :, r * P : (r + 1) * P].rearrange("p t q -> p q t"))
 
-        def multiply(s):
-            if s in DIRECT:
-                for r in range(ROWS):
-                    rows = slice(r * P, (r + 1) * P)
-                    nc.tensor.matmul_mx(out=scores[s][:, r, :], lhsT=q_codes[:, rows].bitcast(FP8X4), lhsT_scale=q_scales[:, rows], rhs=codes[s][:].bitcast(FP8X4), rhs_scale=scales[s][:], start=True, stop=True)
-            else:
-                nc.tensor.matmul_mx(out=scores[s][:].rearrange("p r q -> p (r q)"), lhsT=codes[s][:].bitcast(FP8X4), lhsT_scale=scales[s][:], rhs=q_codes[:].bitcast(FP8X4), rhs_scale=q_scales[:], start=True, stop=True)
+        def quantise_queries(r):
+            nc.vector.quantize_mx(out=q_codes[r][:].bitcast(FP8X4), scales=q_scales[r][:], in_=queries[r][:].rearrange("p q t -> p (q t)"))
 
-        def add_bias(s):
-            if s in DIRECT:
-                nc.vector.tensor_tensor(biased[s][:], scores[s][:], bias_rows[:, DIRECT.index(s), :, :], ADD)
-            else:
-                nc.scalar.activation(biased[s][:], scores[s][:], IDENTITY, bias=bias[:, s : s + 1])
+        def gather(first, count):
+            nc.vector.tensor_copy(keys[:, span(first, count), 3], planes[3][:].indirect(offsets[:, first * CHUNK // 16 : (first + count) * CHUNK // 16]))
 
-        def turn(s, bank):
-            turned[s] = psum.tile([P, ROWS, CHUNK], F32, name="bank%d" % bank)
-            for r in range(ROWS):
-                nc.tensor.transpose(turned[s][:, r, :], biased[s][:, r, :], identity[:])
+        def quantise_keys(first, count):
+            cols = span(first, count)
+            nc.vector.quantize_mx(out=k_codes[:, cols].bitcast(FP8X4), scales=k_scales[:, cols], in_=keys[:, cols, :].rearrange("p n t -> p (n t)"))
 
-        def largest(s):
-            source = biased[s] if s in DIRECT else turned[s]
-            nc.vector.reduce_max(best[:, :, s * PER : (s + 1) * PER], source[:].rearrange("p r (j i) -> p r j i", i=PAGE), axis=mybir.AxisListType.X)
+        def multiply_rows(r, first, count, bank):
+            cols = span(first, count)
+            banks[bank] = psum.tile([P, count * CHUNK], F32, name="bank%d" % bank)
+            nc.tensor.matmul_mx(out=banks[bank][:], lhsT=q_codes[r][:].bitcast(FP8X4), lhsT_scale=q_scales[r][:], rhs=k_codes[:, cols].bitcast(FP8X4), rhs_scale=k_scales[:, cols], start=True, stop=True)
 
-        gather(0)
-        gather(1)
-        quantise(0)
-        quantise(1)
-        quantise(2)
-        quantise(3)
-        multiply(0)
-        multiply(1)
-        add_bias(0)
-        add_bias(1)
-        multiply(2)
-        add_bias(2)
-        multiply(3)
-        turn(1, 4)
-        turn(2, 5)
-        largest(0)
-        add_bias(3)
-        largest(1)
-        largest(3)
-        largest(2)
+        def add_row(r, first, count, bank):
+            cols = span(first, count)
+            nc.vector.tensor_tensor(biased[:, r, cols], banks[bank][:], bias_row[:, cols], ADD)
+
+        def multiply_slots(r, s, bank):
+            cols = span(s, 1)
+            banks[bank] = psum.tile([P, P], F32, name="bank%d" % bank)
+            nc.tensor.matmul_mx(out=banks[bank][:], lhsT=k_codes[:, cols].bitcast(FP8X4), lhsT_scale=k_scales[:, cols], rhs=q_codes[r][:].bitcast(FP8X4), rhs_scale=q_scales[r][:], start=True, stop=True)
+
+        def add_column(r, s, bank):
+            nc.scalar.activation(biased[:, r, span(s, 1)], banks[bank][:], IDENTITY, bias=bias[:, s : s + 1])
+
+        def turn(r, first, count, bank):
+            banks[bank] = psum.tile([P, count * CHUNK], F32, name="bank%d" % bank)
+            for i in range(count):
+                nc.tensor.transpose(banks[bank][:, span(i, 1)], biased[:, r, span(first + i, 1)], identity[:])
+
+        def largest(r, first, count, source):
+            per = CHUNK // PAGE
+            nc.vector.reduce_max(best[:, r, first * per : (first + count) * per], source.rearrange("p (j i) -> p j i", i=PAGE), axis=mybir.AxisListType.X)
+
+        weave(0)
+        weave(1)
+        gather(0, 2)
+        gather(2, 2)
+        quantise_keys(0, 2)
+        quantise_queries(0)
+        quantise_keys(2, 2)
+        quantise_queries(1)
+        multiply_rows(0, 0, 2, 0)
+        multiply_rows(0, 2, 2, 1)
+        multiply_slots(1, 0, 2)
+        multiply_slots(1, 1, 3)
+        multiply_slots(1, 2, 4)
+        multiply_slots(1, 3, 5)
+        add_row(0, 0, 2, 0)
+        add_row(0, 2, 2, 1)
+        add_column(1, 0, 2)
+        add_column(1, 1, 3)
+        add_column(1, 2, 4)
+        add_column(1, 3, 5)
+        turn(1, 0, 2, 6)
+        turn(1, 2, 2, 7)
+        largest(0, 0, 4, biased[:, 0, :])
+        largest(1, 0, 2, banks[6][:])
+        largest(1, 2, 2, banks[7][:])
         nc.sync.dma_start(out[0].rearrange("(r p) j -> p r j", p=P), best[:])

@@ -78,7 +78,7 @@ def tile_attend_maxsim_kb_kernel(tc, qT, kT, kb, offs, out):
             return slice(first * CHUNK, (first + count) * CHUNK)
 
         def weave(r):
-            nc.scalar.copy(queries[r][:], q_raw[:, :, r * P : (r + 1) * P].rearrange("p t q -> p q t"))
+            nc.scalar.copy(queries[r][:].rearrange("p (c i) t -> p c t i", i=4), q_raw[:, :, r * P : (r + 1) * P].rearrange("p t (c i) -> p c t i", i=4))
 
         def quantise_queries(r):
             nc.vector.quantize_mx(out=q_codes[r][:].bitcast(FP8X4), scales=q_scales[r][:], in_=queries[r][:].rearrange("p q t -> p (q t)"))
@@ -138,7 +138,8 @@ def tile_attend_maxsim_kb_kernel(tc, qT, kT, kb, offs, out):
         add_column(1, 3, 5)
         turn(1, 0, 2, 6)
         turn(1, 2, 2, 7)
-        largest(0, 0, 4, biased[:, 0, :])
+        largest(0, 0, 2, biased[:, 0, :HALF])
+        largest(0, 2, 2, biased[:, 0, HALF:])
         largest(1, 0, 2, banks[6][:])
         largest(1, 2, 2, banks[7][:])
         nc.sync.dma_start(out[0].rearrange("(r p) j -> p r j", p=P), best[:])

@@ -48,12 +48,20 @@ def tile_attend_maxsim_kb_kernel(tc, qT, kT, kb, offs, out):
         identity = held.tile([P, P], F32, name="identity")
         make_identity(nc, identity[:])
 
-        keys = held.tile([P, N, PACK], BF16, name="keys", align_bytes=64)
+        early = held.tile([P, HALF * PACK], BF16, name="early", align_bytes=64)
+        late = held.tile([P, 2 * HALF * PACK], BF16, name="late", align_bytes=64)
+        early_words = early[:].rearrange("p (n t) -> p n t", t=PACK)
+        late_words = late[:].rearrange("p (n t) -> p n t", t=PACK)
         kb_listed = held.tile([P, N], F32, name="kb_listed")
-        nc.vector.tensor_copy(keys[:, :, 0], planes[0][:].indirect(offsets[:]))
+
+        def gather(t):
+            nc.vector.tensor_copy(early_words[:, :, t], planes[t][:].indirect(offsets[:, : HALF // 16]))
+            nc.vector.tensor_copy(late_words[:, P : P + HALF, t], planes[t][:].indirect(offsets[:, HALF // 16 :]))
+
+        gather(0)
         nc.vector.tensor_copy(kb_listed[:], kb_row[:].indirect(offsets[:]))
-        for t in (1, 2):
-            nc.vector.tensor_copy(keys[:, :, t], planes[t][:].indirect(offsets[:]))
+        gather(1)
+        gather(2)
         kb_turned = psum.tile([P, CHUNKS, P], F32, name="bank6")
         for s in range(CHUNKS):
             nc.tensor.transpose(kb_turned[:, s, :], kb_listed[:, s * CHUNK : (s + 1) * CHUNK], identity[:])
@@ -66,43 +74,47 @@ def tile_attend_maxsim_kb_kernel(tc, qT, kT, kb, offs, out):
         nc.scalar.copy(bias_row[:], spread[:].rearrange("p s n -> p (s n)"))
 
         best = held.tile([P, ROWS, N // PAGE], F32, name="best")
-        queries = [held.tile([P, P, PACK], BF16, name="queries%d" % r, align_bytes=64) for r in range(ROWS)]
-        q_codes = [held.tile([P, P], U32, name="q_codes%d" % r, align_bytes=64) for r in range(ROWS)]
-        q_scales = [held.tile([P, P], U8, name="q_scales%d" % r, align_bytes=64) for r in range(ROWS)]
-        k_codes = held.tile([P, N], U32, name="k_codes", align_bytes=64)
-        k_scales = held.tile([P, N], U8, name="k_scales", align_bytes=64)
+        early_codes = held.tile([P, HALF], U32, name="early_codes", align_bytes=64)
+        early_scales = held.tile([P, HALF], U8, name="early_scales", align_bytes=64)
+        late_codes = held.tile([P, 2 * HALF], U32, name="late_codes", align_bytes=64)
+        late_scales = held.tile([P, 2 * HALF], U8, name="late_scales", align_bytes=64)
         biased = held.tile([P, ROWS, N], F32, name="biased")
         banks = {}
 
         def span(first, count):
             return slice(first * CHUNK, (first + count) * CHUNK)
 
+        def keys_at(first, count):
+            if first < 2:
+                return early_codes[:, span(first, count)].bitcast(FP8X4), early_scales[:, span(first, count)]
+            return late_codes[:, span(first - 1, count)].bitcast(FP8X4), late_scales[:, span(first - 1, count)]
+
+        def queries_at(r):
+            return late_codes[:, span(3 * r, 1)].bitcast(FP8X4), late_scales[:, span(3 * r, 1)]
+
         def weave(r):
-            nc.scalar.copy(queries[r][:].rearrange("p (c i) t -> p c t i", i=4), q_raw[:, :, r * P : (r + 1) * P].rearrange("p t (c i) -> p c t i", i=4))
+            nc.scalar.copy(late_words[:, span(3 * r, 1), :].rearrange("p (c i) t -> p c t i", i=4), q_raw[:, :, r * P : (r + 1) * P].rearrange("p t (c i) -> p c t i", i=4))
 
-        def quantise_queries(r):
-            nc.vector.quantize_mx(out=q_codes[r][:].bitcast(FP8X4), scales=q_scales[r][:], in_=queries[r][:].rearrange("p q t -> p (q t)"))
+        def quantise_early():
+            nc.vector.quantize_mx(out=early_codes[:].bitcast(FP8X4), scales=early_scales[:], in_=early[:])
 
-        def gather(first, count):
-            nc.vector.tensor_copy(keys[:, span(first, count), 3], planes[3][:].indirect(offsets[:, first * CHUNK // 16 : (first + count) * CHUNK // 16]))
-
-        def quantise_keys(first, count):
-            cols = span(first, count)
-            nc.vector.quantize_mx(out=k_codes[:, cols].bitcast(FP8X4), scales=k_scales[:, cols], in_=keys[:, cols, :].rearrange("p n t -> p (n t)"))
+        def quantise_late(h):
+            cols = span(2 * h, 2)
+            nc.vector.quantize_mx(out=late_codes[:, cols].bitcast(FP8X4), scales=late_scales[:, cols], in_=late[:, h * HALF * PACK : (h + 1) * HALF * PACK])
 
         def multiply_rows(r, first, count, bank):
-            cols = span(first, count)
+            (q, qs), (k, ks) = queries_at(r), keys_at(first, count)
             banks[bank] = psum.tile([P, count * CHUNK], F32, name="bank%d" % bank)
-            nc.tensor.matmul_mx(out=banks[bank][:], lhsT=q_codes[r][:].bitcast(FP8X4), lhsT_scale=q_scales[r][:], rhs=k_codes[:, cols].bitcast(FP8X4), rhs_scale=k_scales[:, cols], start=True, stop=True)
+            nc.tensor.matmul_mx(out=banks[bank][:], lhsT=q, lhsT_scale=qs, rhs=k, rhs_scale=ks, start=True, stop=True)
 
         def add_row(r, first, count, bank):
             cols = span(first, count)
             nc.vector.tensor_tensor(biased[:, r, cols], banks[bank][:], bias_row[:, cols], ADD)
 
         def multiply_slots(r, s, bank):
-            cols = span(s, 1)
+            (q, qs), (k, ks) = queries_at(r), keys_at(s, 1)
             banks[bank] = psum.tile([P, P], F32, name="bank%d" % bank)
-            nc.tensor.matmul_mx(out=banks[bank][:], lhsT=k_codes[:, cols].bitcast(FP8X4), lhsT_scale=k_scales[:, cols], rhs=q_codes[r][:].bitcast(FP8X4), rhs_scale=q_scales[r][:], start=True, stop=True)
+            nc.tensor.matmul_mx(out=banks[bank][:], lhsT=k, lhsT_scale=ks, rhs=q, rhs_scale=qs, start=True, stop=True)
 
         def add_column(r, s, bank):
             nc.scalar.activation(biased[:, r, span(s, 1)], banks[bank][:], IDENTITY, bias=bias[:, s : s + 1])
@@ -118,28 +130,25 @@ def tile_attend_maxsim_kb_kernel(tc, qT, kT, kb, offs, out):
 
         weave(0)
         weave(1)
-        gather(0, 2)
-        gather(2, 2)
-        quantise_keys(0, 2)
-        quantise_queries(0)
-        quantise_keys(2, 2)
-        quantise_queries(1)
+        gather(3)
+        quantise_early()
+        quantise_late(0)
+        quantise_late(1)
         multiply_rows(0, 0, 2, 0)
-        multiply_rows(0, 2, 2, 1)
-        multiply_slots(1, 0, 2)
-        multiply_slots(1, 1, 3)
-        multiply_slots(1, 2, 4)
-        multiply_slots(1, 3, 5)
+        multiply_rows(0, 2, 1, 1)
         add_row(0, 0, 2, 0)
-        add_row(0, 2, 2, 1)
-        add_column(1, 0, 2)
-        add_column(1, 1, 3)
-        add_column(1, 2, 4)
-        add_column(1, 3, 5)
+        add_row(0, 2, 1, 1)
+        for s in range(CHUNKS):
+            multiply_slots(1, s, 2 + s)
+        multiply_rows(0, 3, 1, 0)
+        for s in range(CHUNKS):
+            add_column(1, s, 2 + s)
+        largest(0, 0, 2, biased[:, 0, span(0, 2)])
+        largest(0, 2, 1, biased[:, 0, span(2, 1)])
+        add_row(0, 3, 1, 0)
         turn(1, 0, 2, 6)
         turn(1, 2, 2, 7)
-        largest(0, 0, 2, biased[:, 0, :HALF])
-        largest(0, 2, 2, biased[:, 0, HALF:])
+        largest(0, 3, 1, biased[:, 0, span(3, 1)])
         largest(1, 0, 2, banks[6][:])
         largest(1, 2, 2, banks[7][:])
         nc.sync.dma_start(out[0].rearrange("(r p) j -> p r j", p=P), best[:])

@@ -128,9 +128,14 @@ def tile_attend_maxsim_kb_kernel(tc, qT, kT, kb, offs, out):
             per = CHUNK // PAGE
             nc.vector.reduce_max(best[:, r, first * per : (first + count) * per], source.rearrange("p (j i) -> p j i", i=PAGE), axis=mybir.AxisListType.X)
 
+        last = held.tile([P, N], BF16, name="last")
+        for first, count in ((0, 1), (1, 1), (2, 2)):
+            nc.vector.tensor_copy(last[:, span(first, count)], planes[3][:].indirect(offsets[:, first * CHUNK // 16 : (first + count) * CHUNK // 16]))
+        nc.scalar.copy(early_words[:, span(0, 1), 3], last[:, span(0, 1)])
+        nc.vector.tensor_copy(early_words[:, span(1, 1), 3], last[:, span(1, 1)])
+        nc.vector.tensor_copy(late_words[:, span(1, 2), 3], last[:, span(2, 2)])
         weave(0)
         weave(1)
-        gather(3)
         quantise_early()
         quantise_late(0)
         quantise_late(1)

@@ -10,10 +10,12 @@ CHUNK = 128
 CHUNKS = N // CHUNK
 HALF = N // 2
 ROWS = NQ // P
+SHARE = 64
 
 F32 = mybir.dt.float32
 BF16 = mybir.dt.bfloat16
 U32 = mybir.dt.uint32
+I32 = mybir.dt.int32
 U16 = mybir.dt.uint16
 U8 = mybir.dt.uint8
 FP8X4 = mybir.dt.float8_e4m3fn_x4
@@ -50,18 +52,23 @@ def tile_attend_maxsim_kb_kernel(tc, qT, kT, kb, offs, out):
 
         early = held.tile([P, HALF * PACK], BF16, name="early", align_bytes=64)
         late = held.tile([P, 2 * HALF * PACK], BF16, name="late", align_bytes=64)
-        early_words = early[:].rearrange("p (n t) -> p n t", t=PACK)
         late_words = late[:].rearrange("p (n t) -> p n t", t=PACK)
         kb_listed = held.tile([P, N], F32, name="kb_listed")
 
-        def gather(t):
-            nc.vector.tensor_copy(early_words[:, :, t], planes[t][:].indirect(offsets[:, : HALF // 16]))
-            nc.vector.tensor_copy(late_words[:, P : P + HALF, t], planes[t][:].indirect(offsets[:, HALF // 16 :]))
+        pairs = held.tile([P, N * PACK], BF16, name="pairs")
+        halves = pairs[:].rearrange("p (h n e) -> p h n e", h=2, e=2)
 
-        gather(0)
+        def gather(t, first, stop):
+            nc.vector.tensor_copy(halves[:, t // 2, first:stop, t % 2], planes[t][:].indirect(offsets[:, first // 16 : stop // 16]))
+
+        def join(copy, word, woven, at, first, count):
+            source = pairs[:].bitcast(word).rearrange("p (h n) -> p n h", h=2)[:, first : first + count, :]
+            copy(woven[:].bitcast(word).rearrange("p (n h) -> p n h", h=2)[:, at : at + count, :], source)
+
+        gather(0, 0, N)
         nc.vector.tensor_copy(kb_listed[:], kb_row[:].indirect(offsets[:]))
-        gather(1)
-        gather(2)
+        gather(1, 0, N)
+        gather(2, 0, N)
         kb_turned = psum.tile([P, CHUNKS, P], F32, name="bank6")
         for s in range(CHUNKS):
             nc.tensor.transpose(kb_turned[:, s, :], kb_listed[:, s * CHUNK : (s + 1) * CHUNK], identity[:])
@@ -92,8 +99,9 @@ def tile_attend_maxsim_kb_kernel(tc, qT, kT, kb, offs, out):
         def queries_at(r):
             return late_codes[:, span(3 * r, 1)].bitcast(FP8X4), late_scales[:, span(3 * r, 1)]
 
-        def weave(r):
-            nc.scalar.copy(late_words[:, span(3 * r, 1), :].rearrange("p (c i) t -> p c t i", i=4), q_raw[:, :, r * P : (r + 1) * P].rearrange("p t (c i) -> p c t i", i=4))
+        def weave(copy, first, count):
+            at = first if first < P else first + HALF
+            copy(late_words[:, at : at + count, :].rearrange("p (c i) t -> p c t i", i=4), q_raw[:, :, first : first + count].rearrange("p t (c i) -> p c t i", i=4))
 
         def quantise_early():
             nc.vector.quantize_mx(out=early_codes[:].bitcast(FP8X4), scales=early_scales[:], in_=early[:])
@@ -128,15 +136,15 @@ def tile_attend_maxsim_kb_kernel(tc, qT, kT, kb, offs, out):
             per = CHUNK // PAGE
             nc.vector.reduce_max(best[:, r, first * per : (first + count) * per], source.rearrange("p (j i) -> p j i", i=PAGE), axis=mybir.AxisListType.X)
 
-        last = held.tile([P, N], BF16, name="last")
-        for first, count in ((0, 1), (1, 1), (2, 2)):
-            nc.vector.tensor_copy(last[:, span(first, count)], planes[3][:].indirect(offsets[:, first * CHUNK // 16 : (first + count) * CHUNK // 16]))
-        nc.scalar.copy(early_words[:, span(0, 1), 3], last[:, span(0, 1)])
-        nc.vector.tensor_copy(early_words[:, span(1, 1), 3], last[:, span(1, 1)])
-        nc.vector.tensor_copy(late_words[:, span(1, 2), 3], last[:, span(2, 2)])
-        weave(0)
-        weave(1)
+        gather(3, 0, HALF)
+        gather(3, HALF, N)
+        join(nc.scalar.copy, U32, early, 0, 0, CHUNK)
+        join(nc.vector.tensor_copy, I32, early, CHUNK, CHUNK, CHUNK)
+        join(nc.vector.tensor_copy, I32, late, CHUNK, HALF, HALF)
+        weave(nc.scalar.copy, 0, P)
+        weave(nc.scalar.copy, P, P - SHARE)
         quantise_early()
+        weave(nc.vector.tensor_copy, NQ - SHARE, SHARE)
         quantise_late(0)
         quantise_late(1)
         multiply_rows(0, 0, 2, 0)

@@ -33,18 +33,19 @@ def tile_attend_maxsim_kb_kernel(tc, qT, kT, kb, offs, out):
         psum = ctx.enter_context(tc.psum_pool(name="psum", bufs=1))
 
         offsets = held.tile([P, N // 16], U16, name="offsets")
-        kb_row = held.tile([P, T], F32, name="kb_row")
+        kb_row = held.tile([P, T], F32, name="kb_row", tag="kb_then_pairs")
         nc.gpsimd.memset(kb_row[:, : T // 2], 0.0)
         nc.vector.memset(kb_row[:, T // 2 :], 0.0)
 
         kT_planes = kT.rearrange("(p t) n -> p t n", t=PACK)
-        planes = [held.tile([P, T], F32, name="plane%d" % t) for t in range(PACK)]
+        first_two = held.tile([P, 2 * T], F32, name="first_two")
+        planes = [first_two[:, :T], first_two[:, T:]] + [held.tile([P, T], F32, name="plane%d" % t)[:] for t in range(2, PACK)]
         q_raw = held.tile([P, PACK, NQ], F32, name="q_raw")
-        nc.sync.dma_start(planes[0][:], kT_planes[:, 0, :])
+        nc.sync.dma_start(first_two[:], kT_planes[:, 0:2, :].rearrange("p t n -> p (t n)"))
         nc.sync.dma_start(offsets[:], offs)
         nc.sync.dma_start(kb_row[0:1, :], kb[0:1, :])
-        for t in range(1, PACK):
-            nc.sync.dma_start(planes[t][:], kT_planes[:, t, :])
+        for t in range(2, PACK):
+            nc.sync.dma_start(planes[t], kT_planes[:, t, :])
         nc.sync.dma_start(q_raw[:], qT[0].rearrange("(p t) q -> p t q", t=PACK))
 
         identity = held.tile([P, P], F32, name="identity")
@@ -55,18 +56,18 @@ def tile_attend_maxsim_kb_kernel(tc, qT, kT, kb, offs, out):
         late_words = late[:].rearrange("p (n t) -> p n t", t=PACK)
         kb_listed = held.tile([P, N], F32, name="kb_listed")
 
-        pairs = held.tile([P, N * PACK], BF16, name="pairs")
+        nc.vector.tensor_copy(kb_listed[:], kb_row[:].indirect(offsets[:]))
+        pairs = held.tile([P, N * PACK], BF16, name="pairs", tag="kb_then_pairs")
         halves = pairs[:].rearrange("p (h n e) -> p h n e", h=2, e=2)
 
         def gather(t, first, stop):
-            nc.vector.tensor_copy(halves[:, t // 2, first:stop, t % 2], planes[t][:].indirect(offsets[:, first // 16 : stop // 16]))
+            nc.vector.tensor_copy(halves[:, t // 2, first:stop, t % 2], planes[t].indirect(offsets[:, first // 16 : stop // 16]))
 
         def join(copy, word, woven, at, first, count):
             source = pairs[:].bitcast(word).rearrange("p (h n) -> p n h", h=2)[:, first : first + count, :]
             copy(woven[:].bitcast(word).rearrange("p (n h) -> p n h", h=2)[:, at : at + count, :], source)
 
         gather(0, 0, N)
-        nc.vector.tensor_copy(kb_listed[:], kb_row[:].indirect(offsets[:]))
         gather(1, 0, N)
         gather(2, 0, N)
         kb_turned = psum.tile([P, CHUNKS, P], F32, name="bank6")

@@ -10,7 +10,6 @@ CHUNK = 128
 CHUNKS = N // CHUNK
 HALF = N // 2
 ROWS = NQ // P
-SHARE = 64
 
 F32 = mybir.dt.float32
 BF16 = mybir.dt.bfloat16
@@ -51,9 +50,8 @@ def tile_attend_maxsim_kb_kernel(tc, qT, kT, kb, offs, out):
         identity = held.tile([P, P], F32, name="identity")
         make_identity(nc, identity[:])
 
-        early = held.tile([P, HALF * PACK], BF16, name="early", align_bytes=64)
-        late = held.tile([P, 2 * HALF * PACK], BF16, name="late", align_bytes=64)
-        late_words = late[:].rearrange("p (n t) -> p n t", t=PACK)
+        runs = ["c0","c1","q0","c2","c3","q1"]
+        woven = held.tile([P, len(runs) * CHUNK * PACK], BF16, name="woven", align_bytes=64)
         kb_listed = held.tile([P, N], F32, name="kb_listed")
 
         nc.vector.tensor_copy(kb_listed[:], kb_row[:].indirect(offsets[:]))
@@ -63,7 +61,11 @@ def tile_attend_maxsim_kb_kernel(tc, qT, kT, kb, offs, out):
         def gather(t, first, stop):
             nc.vector.tensor_copy(halves[:, t // 2, first:stop, t % 2], planes[t].indirect(offsets[:, first // 16 : stop // 16]))
 
-        def join(copy, word, woven, at, first, count):
+        def place(kind, first):
+            return runs.index("%s%d" % (kind, first // CHUNK)) * CHUNK + first % CHUNK
+
+        def join(copy, word, first, count):
+            at = place("c", first)
             source = pairs[:].bitcast(word).rearrange("p (h n) -> p n h", h=2)[:, first : first + count, :]
             copy(woven[:].bitcast(word).rearrange("p (n h) -> p n h", h=2)[:, at : at + count, :], source)
 
@@ -82,37 +84,29 @@ def tile_attend_maxsim_kb_kernel(tc, qT, kT, kb, offs, out):
         nc.scalar.copy(bias_row[:], spread[:].rearrange("p s n -> p (s n)"))
 
         best = held.tile([P, ROWS, N // PAGE], F32, name="best")
-        early_codes = held.tile([P, HALF], U32, name="early_codes", align_bytes=64)
-        early_scales = held.tile([P, HALF], U8, name="early_scales", align_bytes=64)
-        late_codes = held.tile([P, 2 * HALF], U32, name="late_codes", align_bytes=64)
-        late_scales = held.tile([P, 2 * HALF], U8, name="late_scales", align_bytes=64)
+        codes = held.tile([P, len(runs) * CHUNK], U32, name="codes", align_bytes=64)
+        scales = held.tile([P, len(runs) * CHUNK], U8, name="scales", align_bytes=64)
         biased = held.tile([P, ROWS, N], F32, name="biased")
+        woven_words = woven[:].rearrange("p (n t) -> p n t", t=PACK)
         banks = {}
 
         def span(first, count):
             return slice(first * CHUNK, (first + count) * CHUNK)
 
-        def keys_at(first, count):
-            if first < 2:
-                return early_codes[:, span(first, count)].bitcast(FP8X4), early_scales[:, span(first, count)]
-            return late_codes[:, span(first - 1, count)].bitcast(FP8X4), late_scales[:, span(first - 1, count)]
-
-        def queries_at(r):
-            return late_codes[:, span(3 * r, 1)].bitcast(FP8X4), late_scales[:, span(3 * r, 1)]
+        def operand(kind, first, count):
+            cols = span(runs.index("%s%d" % (kind, first)), count)
+            return codes[:, cols].bitcast(FP8X4), scales[:, cols]
 
         def weave(copy, first, count):
-            at = first if first < P else first + HALF
-            copy(late_words[:, at : at + count, :].rearrange("p (c i) t -> p c t i", i=4), q_raw[:, :, first : first + count].rearrange("p t (c i) -> p c t i", i=4))
+            at = place("q", first)
+            copy(woven_words[:, at : at + count, :].rearrange("p (c i) t -> p c t i", i=4), q_raw[:, :, first : first + count].rearrange("p t (c i) -> p c t i", i=4))
 
-        def quantise_early():
-            nc.vector.quantize_mx(out=early_codes[:].bitcast(FP8X4), scales=early_scales[:], in_=early[:])
-
-        def quantise_late(h):
-            cols = span(2 * h, 2)
-            nc.vector.quantize_mx(out=late_codes[:, cols].bitcast(FP8X4), scales=late_scales[:, cols], in_=late[:, h * HALF * PACK : (h + 1) * HALF * PACK])
+        def quantise(first, count):
+            cols = span(first, count)
+            nc.vector.quantize_mx(out=codes[:, cols].bitcast(FP8X4), scales=scales[:, cols], in_=woven[:, first * CHUNK * PACK : (first + count) * CHUNK * PACK])
 
         def multiply_rows(r, first, count, bank):
-            (q, qs), (k, ks) = queries_at(r), keys_at(first, count)
+            (q, qs), (k, ks) = operand("q", r, 1), operand("c", first, count)
             banks[bank] = psum.tile([P, count * CHUNK], F32, name="bank%d" % bank)
             nc.tensor.matmul_mx(out=banks[bank][:], lhsT=q, lhsT_scale=qs, rhs=k, rhs_scale=ks, start=True, stop=True)
 
@@ -121,7 +115,7 @@ def tile_attend_maxsim_kb_kernel(tc, qT, kT, kb, offs, out):
             nc.vector.tensor_tensor(biased[:, r, cols], banks[bank][:], bias_row[:, cols], ADD)
 
         def multiply_slots(r, s, bank):
-            (q, qs), (k, ks) = queries_at(r), keys_at(s, 1)
+            (q, qs), (k, ks) = operand("q", r, 1), operand("c", s, 1)
             banks[bank] = psum.tile([P, P], F32, name="bank%d" % bank)
             nc.tensor.matmul_mx(out=banks[bank][:], lhsT=k, lhsT_scale=ks, rhs=q, rhs_scale=qs, start=True, stop=True)
 
@@ -139,30 +133,34 @@ def tile_attend_maxsim_kb_kernel(tc, qT, kT, kb, offs, out):
 
         gather(3, 0, HALF)
         gather(3, HALF, N)
-        join(nc.scalar.copy, U32, early, 0, 0, CHUNK)
-        join(nc.vector.tensor_copy, I32, early, CHUNK, CHUNK, CHUNK)
-        join(nc.vector.tensor_copy, I32, late, CHUNK, HALF, HALF)
+        join(nc.scalar.copy, U32, 0, CHUNK)
+        join(nc.vector.tensor_copy, I32, CHUNK, CHUNK)
+        join(nc.vector.tensor_copy, I32, HALF, HALF)
         weave(nc.scalar.copy, 0, P)
-        weave(nc.scalar.copy, P, P - SHARE)
-        quantise_early()
-        weave(nc.vector.tensor_copy, NQ - SHARE, SHARE)
-        quantise_late(0)
-        quantise_late(1)
+        weave(nc.scalar.copy, P, 64)
+        quantise(0, 2)
+        quantise(3, 1)
+        weave(nc.vector.tensor_copy, P + 64, 64)
+        quantise(2, 1)
+        quantise(4, 2)
         multiply_rows(0, 0, 2, 0)
         multiply_rows(0, 2, 1, 1)
         add_row(0, 0, 2, 0)
         add_row(0, 2, 1, 1)
-        for s in range(CHUNKS):
+        for s in range(3):
             multiply_slots(1, s, 2 + s)
-        multiply_rows(0, 3, 1, 0)
-        for s in range(CHUNKS):
+        last = psum.tile([P, ROWS, CHUNK], F32, name="bank5")
+        for r in range(ROWS):
+            (q, qs), (k, ks) = operand("q", r, 1), operand("c", 3, 1)
+            nc.tensor.matmul_mx(out=last[:, r, :], lhsT=q, lhsT_scale=qs, rhs=k, rhs_scale=ks, start=True, stop=True)
+        for s in range(3):
             add_column(1, s, 2 + s)
         largest(0, 0, 2, biased[:, 0, span(0, 2)])
-        largest(0, 2, 1, biased[:, 0, span(2, 1)])
-        add_row(0, 3, 1, 0)
+        nc.vector.tensor_tensor(biased[:, :, span(3, 1)], last[:], bias_row[:, span(3, 1)].unsqueeze(1).to_broadcast([P, ROWS, CHUNK]), ADD)
         turn(1, 0, 2, 6)
-        turn(1, 2, 2, 7)
-        largest(0, 3, 1, biased[:, 0, span(3, 1)])
+        turn(1, 2, 1, 7)
+        largest(0, 2, 1, biased[:, 0, span(2, 1)])
+        nc.vector.reduce_max(best[:, :, 12:16], biased[:, :, span(3, 1)].rearrange("p r (j i) -> p r j i", i=PAGE), axis=mybir.AxisListType.X)
         largest(1, 0, 2, banks[6][:])
-        largest(1, 2, 2, banks[7][:])
+        largest(1, 2, 1, banks[7][:])
         nc.sync.dma_start(out[0].rearrange("(r p) j -> p r j", p=P), best[:])

@@ -55,7 +55,8 @@ def tile_attend_maxsim_kb_kernel(tc, qT, kT, kb, offs, out):
         kb_listed = held.tile([P, N], F32, name="kb_listed")
 
         nc.vector.tensor_copy(kb_listed[:], kb_row[:].indirect(offsets[:]))
-        pairs = held.tile([P, N * PACK], BF16, name="pairs", tag="kb_then_pairs")
+        listed = held.tile([P, 2, N], F32, name="listed", tag="kb_then_pairs")
+        pairs = held.tile([P, N * PACK], BF16, name="pairs")
         halves = pairs[:].rearrange("p (h n e) -> p h n e", h=2, e=2)
 
         def gather(t, first, stop):
@@ -69,8 +70,8 @@ def tile_attend_maxsim_kb_kernel(tc, qT, kT, kb, offs, out):
             source = pairs[:].bitcast(word).rearrange("p (h n) -> p n h", h=2)[:, first : first + count, :]
             copy(woven[:].bitcast(word).rearrange("p (n h) -> p n h", h=2)[:, at : at + count, :], source)
 
-        gather(0, 0, N)
-        gather(1, 0, N)
+        for t in range(2):
+            nc.vector.tensor_copy(listed[:, t, :], planes[t].indirect(offsets[:]))
         gather(2, 0, N)
         kb_turned = psum.tile([P, CHUNKS, P], F32, name="bank6")
         for s in range(CHUNKS):
@@ -82,6 +83,8 @@ def tile_attend_maxsim_kb_kernel(tc, qT, kT, kb, offs, out):
             nc.tensor.transpose(spread[:, s, :], bias[:, s : s + 1].to_broadcast([P, P]), identity[:])
         bias_row = held.tile([P, N], F32, name="bias_row")
         nc.scalar.copy(bias_row[:], spread[:].rearrange("p s n -> p (s n)"))
+
+        nc.scalar.copy(halves[:, 0].rearrange("p (c i) e -> p c e i", i=4), listed[:].rearrange("p e (c i) -> p c e i", i=4))
 
         best = held.tile([P, ROWS, N // PAGE], F32, name="best")
         codes = held.tile([P, len(runs) * CHUNK], U32, name="codes", align_bytes=64)
@@ -137,10 +140,10 @@ def tile_attend_maxsim_kb_kernel(tc, qT, kT, kb, offs, out):
         join(nc.vector.tensor_copy, I32, CHUNK, CHUNK)
         join(nc.vector.tensor_copy, I32, HALF, HALF)
         weave(nc.scalar.copy, 0, P)
-        weave(nc.scalar.copy, P, 64)
+        weave(nc.scalar.copy, P, P - 40)
         quantise(0, 2)
         quantise(3, 1)
-        weave(nc.vector.tensor_copy, P + 64, 64)
+        weave(nc.vector.tensor_copy, NQ - 40, 40)
         quantise(2, 1)
         quantise(4, 2)
         multiply_rows(0, 0, 2, 0)

@@ -10,6 +10,7 @@ CHUNK = 128
 CHUNKS = N // CHUNK
 HALF = N // 2
 ROWS = NQ // P
+RUN = PAGE // 2
 
 F32 = mybir.dt.float32
 BF16 = mybir.dt.bfloat16
@@ -20,6 +21,7 @@ U8 = mybir.dt.uint8
 FP8X4 = mybir.dt.float8_e4m3fn_x4
 IDENTITY = mybir.ActivationFunctionType.Identity
 ADD = mybir.AluOpType.add
+MAX = mybir.AluOpType.max
 
 FLOPS = 2 * NQ * N * D
 BYTES = 4 * (D * NQ + D * T + T + NQ * N // PAGE) + 2 * P * N // 16
@@ -66,19 +68,25 @@ def tile_attend_maxsim_kb_kernel(tc, qT, kT, kb, offs, out):
             return runs.index("%s%d" % (kind, first // CHUNK)) * CHUNK + first % CHUNK
 
         def join(copy, word, first, count):
-            at = place("c", first)
-            source = pairs[:].bitcast(word).rearrange("p (h n) -> p n h", h=2)[:, first : first + count, :]
-            copy(woven[:].bitcast(word).rearrange("p (n h) -> p n h", h=2)[:, at : at + count, :], source)
+            at = place("c", first * CHUNK)
+            source = pairs[:].bitcast(word).rearrange("p (h g j u i) -> p g u j i h", h=2, g=2, u=2, i=RUN)[:, first // 2, first % 2 : first % 2 + count]
+            target = woven[:].bitcast(word)[:, 2 * at : 2 * (at + count * CHUNK)].rearrange("p (u j i h) -> p u j i h", u=count, i=RUN, h=2)
+            if count == 1:
+                copy(target[:, 0], source[:, 0])
+            else:
+                copy(target, source)
 
         for t in range(2):
             nc.vector.tensor_copy(listed[:, t, :], planes[t].indirect(offsets[:]))
         gather(2, 0, N)
-        kb_turned = psum.tile([P, CHUNKS, P], F32, name="bank6")
+        kb_dealt = held.tile([P, N], F32, name="kb_dealt")
+        nc.scalar.copy(kb_dealt[:].rearrange("p (g u j i) -> p g u j i", g=2, u=2, i=RUN), kb_listed[:].rearrange("p (g j u i) -> p g u j i", g=2, u=2, i=RUN))
+        kb_turned = psum.tile([P, CHUNKS, P], F32, name="bank7")
         for s in range(CHUNKS):
-            nc.tensor.transpose(kb_turned[:, s, :], kb_listed[:, s * CHUNK : (s + 1) * CHUNK], identity[:])
+            nc.tensor.transpose(kb_turned[:, s, :], kb_dealt[:, s * CHUNK : (s + 1) * CHUNK], identity[:])
         bias = held.tile([P, CHUNKS], F32, name="bias")
         nc.scalar.copy(bias[:], kb_turned[:, :, 0])
-        spread = psum.tile([P, CHUNKS, P], F32, name="bank7")
+        spread = psum.tile([P, CHUNKS, P], F32, name="bank6")
         for s in range(CHUNKS):
             nc.tensor.transpose(spread[:, s, :], bias[:, s : s + 1].to_broadcast([P, P]), identity[:])
         bias_row = held.tile([P, N], F32, name="bias_row")
@@ -89,9 +97,10 @@ def tile_attend_maxsim_kb_kernel(tc, qT, kT, kb, offs, out):
         best = held.tile([P, ROWS, N // PAGE], F32, name="best")
         codes = held.tile([P, len(runs) * CHUNK], U32, name="codes", align_bytes=64)
         scales = held.tile([P, len(runs) * CHUNK], U8, name="scales", align_bytes=64)
-        biased = held.tile([P, ROWS, N], F32, name="biased")
         woven_words = woven[:].rearrange("p (n t) -> p n t", t=PACK)
         banks = {}
+        biased = {}
+        larger = {}
 
         def span(first, count):
             return slice(first * CHUNK, (first + count) * CHUNK)
@@ -108,62 +117,59 @@ def tile_attend_maxsim_kb_kernel(tc, qT, kT, kb, offs, out):
             cols = span(first, count)
             nc.vector.quantize_mx(out=codes[:, cols].bitcast(FP8X4), scales=scales[:, cols], in_=woven[:, first * CHUNK * PACK : (first + count) * CHUNK * PACK])
 
-        def multiply_rows(r, first, count, bank):
-            (q, qs), (k, ks) = operand("q", r, 1), operand("c", first, count)
-            banks[bank] = psum.tile([P, count * CHUNK], F32, name="bank%d" % bank)
-            nc.tensor.matmul_mx(out=banks[bank][:], lhsT=q, lhsT_scale=qs, rhs=k, rhs_scale=ks, start=True, stop=True)
+        def multiply(r, s, n=1):
+            (q, qs), (k, ks) = operand("q", r, n), operand("c", s, 1)
+            banks[r, s] = psum.tile([P, n * P], F32, name="bank%d" % (CHUNKS * r + s))
+            nc.tensor.matmul_mx(out=banks[r, s][:], lhsT=k, lhsT_scale=ks, rhs=q, rhs_scale=qs, start=True, stop=True)
 
-        def add_row(r, first, count, bank):
-            cols = span(first, count)
-            nc.vector.tensor_tensor(biased[:, r, cols], banks[bank][:], bias_row[:, cols], ADD)
+        def add_bias(r, g, n=1):
+            biased[r, g] = held.tile([P, n * P], F32, name="biased%d%d" % (r, g))
+            nc.scalar.activation(biased[r, g][:], banks[r, 2 * g][:], IDENTITY, bias=bias[:, 2 * g : 2 * g + 1])
 
-        def multiply_slots(r, s, bank):
-            (q, qs), (k, ks) = operand("q", r, 1), operand("c", s, 1)
-            banks[bank] = psum.tile([P, P], F32, name="bank%d" % bank)
-            nc.tensor.matmul_mx(out=banks[bank][:], lhsT=k, lhsT_scale=ks, rhs=q, rhs_scale=qs, start=True, stop=True)
-
-        def add_column(r, s, bank):
-            nc.scalar.activation(biased[:, r, span(s, 1)], banks[bank][:], IDENTITY, bias=bias[:, s : s + 1])
-
-        def turn(r, first, count, bank):
-            banks[bank] = psum.tile([P, count * CHUNK], F32, name="bank%d" % bank)
-            for i in range(count):
-                nc.tensor.transpose(banks[bank][:, span(i, 1)], biased[:, r, span(first + i, 1)], identity[:])
-
-        def largest(r, first, count, source):
-            per = CHUNK // PAGE
-            nc.vector.reduce_max(best[:, r, first * per : (first + count) * per], source.rearrange("p (j i) -> p j i", i=PAGE), axis=mybir.AxisListType.X)
+        def take_larger(r, g, n=1):
+            larger[r, g] = held.tile([P, n * P], F32, name="larger%d%d" % (r, g))
+            nc.vector.scalar_tensor_tensor(larger[r, g][:], banks[r, 2 * g + 1][:], bias[:, 2 * g + 1 : 2 * g + 2], biased[r, g][:], ADD, MAX)
 
         gather(3, 0, HALF)
         gather(3, HALF, N)
-        join(nc.scalar.copy, U32, 0, CHUNK)
-        join(nc.vector.tensor_copy, I32, CHUNK, CHUNK)
-        join(nc.vector.tensor_copy, I32, HALF, HALF)
+        join(nc.scalar.copy, U32, 0, 1)
+        join(nc.vector.tensor_copy, I32, 1, 1)
+        join(nc.vector.tensor_copy, I32, 2, 2)
         weave(nc.scalar.copy, 0, P)
-        weave(nc.scalar.copy, P, P - 40)
+        weave(nc.scalar.copy, P, P)
         quantise(0, 2)
         quantise(3, 1)
-        weave(nc.vector.tensor_copy, NQ - 40, 40)
         quantise(2, 1)
         quantise(4, 2)
-        multiply_rows(0, 0, 2, 0)
-        multiply_rows(0, 2, 1, 1)
-        add_row(0, 0, 2, 0)
-        add_row(0, 2, 1, 1)
-        for s in range(3):
-            multiply_slots(1, s, 2 + s)
-        last = psum.tile([P, ROWS, CHUNK], F32, name="bank5")
-        for r in range(ROWS):
-            (q, qs), (k, ks) = operand("q", r, 1), operand("c", 3, 1)
-            nc.tensor.matmul_mx(out=last[:, r, :], lhsT=q, lhsT_scale=qs, rhs=k, rhs_scale=ks, start=True, stop=True)
-        for s in range(3):
-            add_column(1, s, 2 + s)
-        largest(0, 0, 2, biased[:, 0, span(0, 2)])
-        nc.vector.tensor_tensor(biased[:, :, span(3, 1)], last[:], bias_row[:, span(3, 1)].unsqueeze(1).to_broadcast([P, ROWS, CHUNK]), ADD)
-        turn(1, 0, 2, 6)
-        turn(1, 2, 1, 7)
-        largest(0, 2, 1, biased[:, 0, span(2, 1)])
-        nc.vector.reduce_max(best[:, :, 12:16], biased[:, :, span(3, 1)].rearrange("p r (j i) -> p r j i", i=PAGE), axis=mybir.AxisListType.X)
-        largest(1, 0, 2, banks[6][:])
-        largest(1, 2, 1, banks[7][:])
+        def multiply_rows(r, g, bank):
+            (q, qs), (k, ks) = operand("q", r, 1), operand("c", 2 * g, 2)
+            banks[r, g, "rows"] = psum.tile([P, HALF], F32, name="bank%d" % bank)
+            nc.tensor.matmul_mx(out=banks[r, g, "rows"][:], lhsT=q, lhsT_scale=qs, rhs=k, rhs_scale=ks, start=True, stop=True)
+
+        def add_row(r, g):
+            biased[r, g] = held.tile([P, HALF], F32, name="biased%d%d" % (r, g))
+            nc.vector.tensor_tensor(biased[r, g][:], banks[r, g, "rows"][:], bias_row[:, g * HALF : (g + 1) * HALF], ADD)
+
+        def largest(r, g):
+            nc.vector.reduce_max(best[:, r, 8 * g : 8 * (g + 1)], biased[r, g][:].rearrange("p (u j i) -> p j u i", u=2, i=RUN), axis=mybir.AxisListType.XY)
+
+        def finish(r, first, count, bank):
+            turned = psum.tile([P, count, P], F32, name="bank%d" % bank)
+            for g in range(count):
+                nc.tensor.transpose(turned[:, g, :], larger[r, first + g][:], identity[:])
+            nc.vector.reduce_max(best[:, r, 8 * first : 8 * (first + count)], turned[:].rearrange("p g (j i) -> p (g j) i", i=RUN), axis=mybir.AxisListType.X)
+
+        for s in (0, 2, 1, 3):
+            multiply(0, s)
+        multiply_rows(1, 0, 4)
+        multiply_rows(1, 1, 5)
+        add_bias(0, 0)
+        add_bias(0, 1)
+        take_larger(0, 0)
+        take_larger(0, 1)
+        add_row(1, 0)
+        add_row(1, 1)
+        largest(1, 0)
+        largest(1, 1)
+        finish(0, 0, 2, 0)
         nc.sync.dma_start(out[0].rearrange("(r p) j -> p r j", p=P), best[:])

@@ -59,18 +59,18 @@ def tile_attend_maxsim_kb_kernel(tc, qT, kT, kb, offs, out):
         nc.vector.tensor_copy(kb_listed[:], kb_row[:].indirect(offsets[:]))
         listed = held.tile([P, 2, N], F32, name="listed", tag="kb_then_pairs")
         pairs = held.tile([P, N * PACK], BF16, name="pairs")
-        halves = pairs[:].rearrange("p (h n e) -> p h n e", h=2, e=2)
+        halves = pairs[:].rearrange("p (h u m e) -> p h m u e", h=2, u=2, e=2)
 
         def gather(t, first, stop):
-            nc.vector.tensor_copy(halves[:, t // 2, first:stop, t % 2], planes[t].indirect(offsets[:, first // 16 : stop // 16]))
+            nc.vector.tensor_copy(halves[:, t // 2, first // 2 : stop // 2, :, t % 2], planes[t].indirect(offsets[:, first // 16 : stop // 16]))
 
         def place(kind, first):
             return runs.index("%s%d" % (kind, first // CHUNK)) * CHUNK + first % CHUNK
 
         def join(copy, word, first, count):
             at = place("c", first * CHUNK)
-            source = pairs[:].bitcast(word).rearrange("p (h g j u i) -> p g u j i h", h=2, g=2, u=2, i=RUN)[:, first // 2, first % 2 : first % 2 + count]
-            target = woven[:].bitcast(word)[:, 2 * at : 2 * (at + count * CHUNK)].rearrange("p (u j i h) -> p u j i h", u=count, i=RUN, h=2)
+            source = pairs[:].bitcast(word).rearrange("p (h u g m) -> p g u m h", h=2, u=2, g=2)[:, first // 2, first % 2 : first % 2 + count]
+            target = woven[:].bitcast(word)[:, 2 * at : 2 * (at + count * CHUNK)].rearrange("p (u m h) -> p u m h", u=count, h=2)
             if count == 1:
                 copy(target[:, 0], source[:, 0])
             else:
@@ -79,11 +79,9 @@ def tile_attend_maxsim_kb_kernel(tc, qT, kT, kb, offs, out):
         for t in range(2):
             nc.vector.tensor_copy(listed[:, t, :], planes[t].indirect(offsets[:]))
         gather(2, 0, N)
-        kb_dealt = held.tile([P, N], F32, name="kb_dealt")
-        nc.scalar.copy(kb_dealt[:].rearrange("p (g u j i) -> p g u j i", g=2, u=2, i=RUN), kb_listed[:].rearrange("p (g j u i) -> p g u j i", g=2, u=2, i=RUN))
         kb_turned = psum.tile([P, CHUNKS, P], F32, name="bank7")
         for s in range(CHUNKS):
-            nc.tensor.transpose(kb_turned[:, s, :], kb_dealt[:, s * CHUNK : (s + 1) * CHUNK], identity[:])
+            nc.tensor.transpose(kb_turned[:, s, :], kb_listed[:, s // 2 * HALF + s % 2 : (s // 2 + 1) * HALF : 2], identity[:])
         bias = held.tile([P, CHUNKS], F32, name="bias")
         nc.scalar.copy(bias[:], kb_turned[:, :, 0])
         spread = psum.tile([P, CHUNKS, P], F32, name="bank6")
@@ -92,7 +90,7 @@ def tile_attend_maxsim_kb_kernel(tc, qT, kT, kb, offs, out):
         bias_row = held.tile([P, N], F32, name="bias_row")
         nc.scalar.copy(bias_row[:], spread[:].rearrange("p s n -> p (s n)"))
 
-        nc.scalar.copy(halves[:, 0].rearrange("p (c i) e -> p c e i", i=4), listed[:].rearrange("p e (c i) -> p c e i", i=4))
+        nc.scalar.copy(halves[:, 0].rearrange("p (c i) u e -> p c e i u", i=4), listed[:].rearrange("p e (c i u) -> p c e i u", i=4, u=2))
 
         best = held.tile([P, ROWS, N // PAGE], F32, name="best")
         codes = held.tile([P, len(runs) * CHUNK], U32, name="codes", align_bytes=64)

@@ -82,8 +82,10 @@ def tile_attend_maxsim_kb_kernel(tc, qT, kT, kb, offs, out):
         kb_turned = psum.tile([P, CHUNKS, P], F32, name="bank7")
         for s in range(CHUNKS):
             nc.tensor.transpose(kb_turned[:, s, :], kb_listed[:, s // 2 * HALF + s % 2 : (s // 2 + 1) * HALF : 2], identity[:])
+        bias_even = held.tile([P, 2], F32, name="bias_even", tag="bias_then_sums")
         bias = held.tile([P, CHUNKS], F32, name="bias")
         nc.scalar.copy(bias[:], kb_turned[:, :, 0])
+        nc.scalar.copy(bias_even[:], bias[:, 0:CHUNKS:2])
         spread = psum.tile([P, CHUNKS, P], F32, name="bank6")
         for s in range(CHUNKS):
             nc.tensor.transpose(spread[:, s, :], bias[:, s : s + 1].to_broadcast([P, P]), identity[:])
@@ -122,7 +124,7 @@ def tile_attend_maxsim_kb_kernel(tc, qT, kT, kb, offs, out):
 
         def add_bias(r, g, n=1):
             biased[r, g] = held.tile([P, n * P], F32, name="biased%d%d" % (r, g))
-            nc.scalar.activation(biased[r, g][:], banks[r, 2 * g][:], IDENTITY, bias=bias[:, 2 * g : 2 * g + 1])
+            nc.scalar.activation(biased[r, g][:], banks[r, 2 * g][:], IDENTITY, bias=bias_even[:, g : g + 1])
 
         def take_larger(r, g, n=1):
             larger[r, g] = held.tile([P, n * P], F32, name="larger%d%d" % (r, g))
@@ -136,16 +138,16 @@ def tile_attend_maxsim_kb_kernel(tc, qT, kT, kb, offs, out):
         weave(nc.scalar.copy, 0, P)
         weave(nc.scalar.copy, P, P)
         quantise(0, 2)
-        quantise(3, 1)
+        quantise(3, 2)
         quantise(2, 1)
-        quantise(4, 2)
+        quantise(5, 1)
         def multiply_rows(r, g, bank):
             (q, qs), (k, ks) = operand("q", r, 1), operand("c", 2 * g, 2)
             banks[r, g, "rows"] = psum.tile([P, HALF], F32, name="bank%d" % bank)
             nc.tensor.matmul_mx(out=banks[r, g, "rows"][:], lhsT=q, lhsT_scale=qs, rhs=k, rhs_scale=ks, start=True, stop=True)
 
         def add_row(r, g):
-            biased[r, g] = held.tile([P, HALF], F32, name="biased%d%d" % (r, g))
+            biased[r, g] = held.tile([P, HALF], F32, name="biased%d%d" % (r, g), tag="bias_then_sums" if g == 0 else "sums")
             nc.vector.tensor_tensor(biased[r, g][:], banks[r, g, "rows"][:], bias_row[:, g * HALF : (g + 1) * HALF], ADD)
 
         def largest(r, g):

@@ -52,8 +52,9 @@ def tile_attend_maxsim_kb_kernel(tc, qT, kT, kb, offs, out):
         identity = held.tile([P, P], F32, name="identity")
         make_identity(nc, identity[:])
 
-        runs = ["c0","c1","q0","c2","c3","q1"]
-        woven = held.tile([P, len(runs) * CHUNK * PACK], BF16, name="woven", align_bytes=64)
+        runs = ["c0","c1","c2","c3","q1","q0"]
+        woven = held.tile([P, (len(runs) - 1) * CHUNK * PACK], BF16, name="woven", align_bytes=64)
+        woven_first = held.tile([P, CHUNK * PACK], BF16, name="woven_first", tag="first_rows_then_codes", align_bytes=64)
         kb_listed = held.tile([P, N], F32, name="kb_listed")
 
         nc.vector.tensor_copy(kb_listed[:], kb_row[:].indirect(offsets[:]))
@@ -107,7 +108,8 @@ def tile_attend_maxsim_kb_kernel(tc, qT, kT, kb, offs, out):
 
         def operand(kind, first, count):
             cols = span(runs.index("%s%d" % (kind, first)), count)
-            return codes[:, cols].bitcast(FP8X4), scales[:, cols]
+            words = last_codes[:] if (kind, first) == ("c", 3) else codes[:, cols]
+            return words.bitcast(FP8X4), scales[:, cols]
 
         def weave(copy, first, count):
             at = place("q", first)
@@ -135,12 +137,14 @@ def tile_attend_maxsim_kb_kernel(tc, qT, kT, kb, offs, out):
         join(nc.scalar.copy, U32, 0, 1)
         join(nc.vector.tensor_copy, I32, 1, 1)
         join(nc.vector.tensor_copy, I32, 2, 2)
-        weave(nc.scalar.copy, 0, P)
+        nc.scalar.copy(woven_first[:].rearrange("p (c i t) -> p c t i", i=4, t=PACK), q_raw[:, :, :P].rearrange("p t (c i) -> p c t i", i=4))
         weave(nc.scalar.copy, P, P)
         quantise(0, 2)
-        quantise(3, 2)
         quantise(2, 1)
-        quantise(5, 1)
+        nc.vector.quantize_mx(out=codes[:, span(5, 1)].bitcast(FP8X4), scales=scales[:, span(5, 1)], in_=woven_first[:])
+        last_codes = held.tile([P, CHUNK], U32, name="last_codes", tag="first_rows_then_codes", align_bytes=64)
+        nc.vector.quantize_mx(out=last_codes[:].bitcast(FP8X4), scales=scales[:, span(3, 1)], in_=woven[:, 3 * CHUNK * PACK : 4 * CHUNK * PACK])
+        quantise(4, 1)
         def multiply_rows(r, g, bank):
             (q, qs), (k, ks) = operand("q", r, 1), operand("c", 2 * g, 2)
             banks[r, g, "rows"] = psum.tile([P, HALF], F32, name="bank%d" % bank)
@@ -162,7 +166,10 @@ def tile_attend_maxsim_kb_kernel(tc, qT, kT, kb, offs, out):
         for s in (0, 2, 1, 3):
             multiply(0, s)
         multiply_rows(1, 0, 4)
-        multiply_rows(1, 1, 5)
+        banks[1, 1, "rows"] = psum.tile([P, HALF], F32, name="bank5")
+        for s in range(2):
+            (q, qs), (k, ks) = operand("q", 1, 1), operand("c", 2 + s, 1)
+            nc.tensor.matmul_mx(out=banks[1, 1, "rows"][:, span(s, 1)], lhsT=q, lhsT_scale=qs, rhs=k, rhs_scale=ks, start=True, stop=True)
         add_bias(0, 0)
         add_bias(0, 1)
         take_larger(0, 0)

@@ -49,6 +49,8 @@ def tile_attend_maxsim_kb_kernel(tc, qT, kT, kb, offs, out):
             nc.sync.dma_start(planes[t], kT_planes[:, t, :])
         nc.sync.dma_start(q_raw[:], qT[0].rearrange("(p t) q -> p t q", t=PACK))
 
+        q_dealt = q_raw[:].rearrange("p t (c i r) -> p r c t i", i=4, r=ROWS)
+
         identity = held.tile([P, P], F32, name="identity")
         make_identity(nc, identity[:])
 
@@ -113,7 +115,7 @@ def tile_attend_maxsim_kb_kernel(tc, qT, kT, kb, offs, out):
 
         def weave(copy, first, count):
             at = place("q", first)
-            copy(woven_words[:, at : at + count, :].rearrange("p (c i) t -> p c t i", i=4), q_raw[:, :, first : first + count].rearrange("p t (c i) -> p c t i", i=4))
+            copy(woven_words[:, at : at + count, :].rearrange("p (c i) t -> p c t i", i=4), q_dealt[:, first // P])
 
         def quantise(first, count):
             cols = span(first, count)
@@ -137,7 +139,7 @@ def tile_attend_maxsim_kb_kernel(tc, qT, kT, kb, offs, out):
         join(nc.scalar.copy, U32, 0, 1)
         join(nc.vector.tensor_copy, I32, 1, 1)
         join(nc.vector.tensor_copy, I32, 2, 2)
-        nc.scalar.copy(woven_first[:].rearrange("p (c i t) -> p c t i", i=4, t=PACK), q_raw[:, :, :P].rearrange("p t (c i) -> p c t i", i=4))
+        nc.scalar.copy(woven_first[:].rearrange("p (c i t) -> p c t i", i=4, t=PACK), q_dealt[:, 0])
         weave(nc.scalar.copy, P, P)
         quantise(0, 2)
         quantise(2, 1)
@@ -179,4 +181,4 @@ def tile_attend_maxsim_kb_kernel(tc, qT, kT, kb, offs, out):
         largest(1, 0)
         largest(1, 1)
         finish(0, 0, 2, 0)
-        nc.sync.dma_start(out[0].rearrange("(r p) j -> p r j", p=P), best[:])
+        nc.sync.dma_start(out[0].rearrange("(p r) j -> p (r j)", r=ROWS), best[:].rearrange("p r j -> p (r j)"))

@@ -19,6 +19,7 @@ I32 = mybir.dt.int32
 U16 = mybir.dt.uint16
 U8 = mybir.dt.uint8
 FP8X4 = mybir.dt.float8_e4m3fn_x4
+COPY = mybir.ActivationFunctionType.Copy
 IDENTITY = mybir.ActivationFunctionType.Identity
 ADD = mybir.AluOpType.add
 MAX = mybir.AluOpType.max
@@ -51,8 +52,10 @@ def tile_attend_maxsim_kb_kernel(tc, qT, kT, kb, offs, out):
 
         q_dealt = q_raw[:].rearrange("p t (c i r) -> p r c t i", i=4, r=ROWS)
 
+        narrow_identity = held.tile([P, P], BF16, name="narrow_identity", tag="identity_then_listed")
+        make_identity(nc, narrow_identity[:])
         identity = held.tile([P, P], F32, name="identity")
-        make_identity(nc, identity[:])
+        nc.scalar.copy(identity[:], narrow_identity[:])
 
         runs = ["c0","c1","c2","c3","q1","q0"]
         woven = held.tile([P, (len(runs) - 1) * CHUNK * PACK], BF16, name="woven", align_bytes=64)
@@ -60,8 +63,8 @@ def tile_attend_maxsim_kb_kernel(tc, qT, kT, kb, offs, out):
         kb_listed = held.tile([P, N], F32, name="kb_listed")
 
         nc.vector.tensor_copy(kb_listed[:], kb_row[:].indirect(offsets[:]))
-        listed = held.tile([P, 2, N], F32, name="listed", tag="kb_then_pairs")
-        pairs = held.tile([P, N * PACK], BF16, name="pairs")
+        listed = held.tile([P, 2, N], F32, name="listed", tag="identity_then_listed")
+        pairs = held.tile([P, N * PACK], BF16, name="pairs", tag="kb_then_pairs")
         halves = pairs[:].rearrange("p (h u m e) -> p h m u e", h=2, u=2, e=2)
 
         def gather(t, first, stop):
@@ -79,8 +82,8 @@ def tile_attend_maxsim_kb_kernel(tc, qT, kT, kb, offs, out):
             else:
                 copy(target, source)
 
-        for t in range(2):
-            nc.vector.tensor_copy(listed[:, t, :], planes[t].indirect(offsets[:]))
+        nc.scalar.activation(listed[:, 0, :], first_two[:].indirect(offsets[:]), COPY)
+        nc.vector.tensor_copy(listed[:, 1, :], planes[1].indirect(offsets[:]))
         gather(2, 0, N)
         kb_turned = psum.tile([P, CHUNKS, P], F32, name="bank7")
         for s in range(CHUNKS):

@@ -40,9 +40,9 @@ def tile_attend_maxsim_kb_kernel(tc, qT, kT, kb, offs, out):
         nc.vector.memset(kb_row[:, T // 2 :], 0.0)
 
         kT_planes = kT.rearrange("(p t) n -> p t n", t=PACK)
-        first_two = held.tile([P, 2 * T], F32, name="first_two")
-        planes = [first_two[:, :T], first_two[:, T:]] + [held.tile([P, T], F32, name="plane%d" % t)[:] for t in range(2, PACK)]
-        q_raw = held.tile([P, PACK, NQ], F32, name="q_raw")
+        first_two = held.tile([P, 2 * T], F32, name="first_two", align_bytes=256)
+        planes = [first_two[:, :T], first_two[:, T:]] + [held.tile([P, T], F32, name="plane%d" % t, align_bytes=256)[:] for t in range(2, PACK)]
+        q_raw = held.tile([P, PACK, NQ], F32, name="q_raw", align_bytes=256)
         nc.sync.dma_start(first_two[:], kT_planes[:, 0:2, :].rearrange("p t n -> p (t n)"))
         nc.sync.dma_start(offsets[:], offs)
         nc.sync.dma_start(kb_row[0:1, :], kb[0:1, :])

from contextlib import ExitStack

import concourse.mybir as mybir
from concourse.masks import make_identity

D, T, N, NQ, PAGE = 512, 2048, 512, 256, 32
P = 128
PACK = 4
CHUNK = 128
CHUNKS = N // CHUNK
HALF = N // 2
ROWS = NQ // P
RUN = PAGE // 2

F32 = mybir.dt.float32
BF16 = mybir.dt.bfloat16
U32 = mybir.dt.uint32
I32 = mybir.dt.int32
U16 = mybir.dt.uint16
U8 = mybir.dt.uint8
FP8X4 = mybir.dt.float8_e4m3fn_x4
COPY = mybir.ActivationFunctionType.Copy
IDENTITY = mybir.ActivationFunctionType.Identity
ADD = mybir.AluOpType.add
MAX = mybir.AluOpType.max

FLOPS = 2 * NQ * N * D
BYTES = 4 * (D * NQ + D * T + T + NQ * N // PAGE) + 2 * P * N // 16


def tile_attend_maxsim_kb_kernel(tc, qT, kT, kb, offs, out):
    nc = tc.nc
    with ExitStack() as ctx:
        held = ctx.enter_context(tc.tile_pool(name="held", bufs=1))
        psum = ctx.enter_context(tc.psum_pool(name="psum", bufs=1))

        offsets = held.tile([P, N // 16], U16, name="offsets")
        kb_row = held.tile([P, T], F32, name="kb_row", tag="kb_then_pairs")
        nc.gpsimd.memset(kb_row[:, : T // 2], 0.0)
        nc.vector.memset(kb_row[:, T // 2 :], 0.0)

        kT_planes = kT.rearrange("(p t) n -> p t n", t=PACK)
        first_two = held.tile([P, 2 * T], F32, name="first_two", align_bytes=256)
        planes = [first_two[:, :T], first_two[:, T:]] + [held.tile([P, T], F32, name="plane%d" % t, align_bytes=256)[:] for t in range(2, PACK)]
        q_raw = held.tile([P, PACK, NQ], F32, name="q_raw", align_bytes=256)
        nc.sync.dma_start(first_two[:], kT_planes[:, 0:2, :].rearrange("p t n -> p (t n)"))
        nc.sync.dma_start(offsets[:], offs)
        nc.sync.dma_start(kb_row[0:1, :], kb[0:1, :])
        for t in range(2, PACK):
            nc.sync.dma_start(planes[t], kT_planes[:, t, :])
        nc.sync.dma_start(q_raw[:], qT[0].rearrange("(p t) q -> p t q", t=PACK))

        q_dealt = q_raw[:].rearrange("p t (c i r) -> p r c t i", i=4, r=ROWS)

        narrow_identity = held.tile([P, P], BF16, name="narrow_identity", tag="identity_then_listed")
        make_identity(nc, narrow_identity[:])
        identity = held.tile([P, P], F32, name="identity")
        nc.scalar.copy(identity[:], narrow_identity[:])

        runs = ["c0","c1","c2","c3","q1","q0"]
        woven = held.tile([P, (len(runs) - 1) * CHUNK * PACK], BF16, name="woven", align_bytes=64)
        woven_first = held.tile([P, CHUNK * PACK], BF16, name="woven_first", tag="first_rows_then_codes", align_bytes=64)
        kb_listed = held.tile([P, N], F32, name="kb_listed")

        nc.vector.tensor_copy(kb_listed[:], kb_row[:].indirect(offsets[:]))
        listed = held.tile([P, 2, N], F32, name="listed", tag="identity_then_listed")
        pairs = held.tile([P, N * PACK], BF16, name="pairs", tag="kb_then_pairs")
        halves = pairs[:].rearrange("p (h u m e) -> p h m u e", h=2, u=2, e=2)

        def gather(t, first, stop):
            nc.vector.tensor_copy(halves[:, t // 2, first // 2 : stop // 2, :, t % 2], planes[t].indirect(offsets[:, first // 16 : stop // 16]))

        def place(kind, first):
            return runs.index("%s%d" % (kind, first // CHUNK)) * CHUNK + first % CHUNK

        def join(copy, word, first, count):
            at = place("c", first * CHUNK)
            source = pairs[:].bitcast(word).rearrange("p (h u g m) -> p g u m h", h=2, u=2, g=2)[:, first // 2, first % 2 : first % 2 + count]
            target = woven[:].bitcast(word)[:, 2 * at : 2 * (at + count * CHUNK)].rearrange("p (u m h) -> p u m h", u=count, h=2)
            if count == 1:
                copy(target[:, 0], source[:, 0])
            else:
                copy(target, source)

        nc.scalar.activation(listed[:, 0, :], first_two[:].indirect(offsets[:]), COPY)
        nc.vector.tensor_copy(listed[:, 1, :], planes[1].indirect(offsets[:]))
        gather(2, 0, N)
        kb_turned = psum.tile([P, CHUNKS, P], F32, name="bank7")
        for s in range(CHUNKS):
            nc.tensor.transpose(kb_turned[:, s, :], kb_listed[:, s // 2 * HALF + s % 2 : (s // 2 + 1) * HALF : 2], identity[:])
        bias_even = held.tile([P, 2], F32, name="bias_even", tag="bias_then_sums")
        bias = held.tile([P, CHUNKS], F32, name="bias")
        nc.scalar.copy(bias[:], kb_turned[:, :, 0])
        nc.scalar.copy(bias_even[:], bias[:, 0:CHUNKS:2])
        spread = psum.tile([P, CHUNKS, P], F32, name="bank6")
        for s in range(CHUNKS):
            nc.tensor.transpose(spread[:, s, :], bias[:, s : s + 1].to_broadcast([P, P]), identity[:])
        bias_row = held.tile([P, N], F32, name="bias_row")
        nc.scalar.copy(bias_row[:], spread[:].rearrange("p s n -> p (s n)"))

        nc.scalar.copy(halves[:, 0].rearrange("p (c i) u e -> p c e i u", i=4), listed[:].rearrange("p e (c i u) -> p c e i u", i=4, u=2))

        best = held.tile([P, ROWS, N // PAGE], F32, name="best")
        codes = held.tile([P, len(runs) * CHUNK], U32, name="codes", align_bytes=64)
        scales = held.tile([P, len(runs) * CHUNK], U8, name="scales", align_bytes=64)
        woven_words = woven[:].rearrange("p (n t) -> p n t", t=PACK)
        banks = {}
        biased = {}
        larger = {}

        def span(first, count):
            return slice(first * CHUNK, (first + count) * CHUNK)

        def operand(kind, first, count):
            cols = span(runs.index("%s%d" % (kind, first)), count)
            words = last_codes[:] if (kind, first) == ("c", 3) else codes[:, cols]
            return words.bitcast(FP8X4), scales[:, cols]

        def weave(copy, first, count):
            at = place("q", first)
            copy(woven_words[:, at : at + count, :].rearrange("p (c i) t -> p c t i", i=4), q_dealt[:, first // P])

        def quantise(first, count):
            cols = span(first, count)
            nc.vector.quantize_mx(out=codes[:, cols].bitcast(FP8X4), scales=scales[:, cols], in_=woven[:, first * CHUNK * PACK : (first + count) * CHUNK * PACK])

        def multiply(r, s, n=1):
            (q, qs), (k, ks) = operand("q", r, n), operand("c", s, 1)
            banks[r, s] = psum.tile([P, n * P], F32, name="bank%d" % (CHUNKS * r + s))
            nc.tensor.matmul_mx(out=banks[r, s][:], lhsT=k, lhsT_scale=ks, rhs=q, rhs_scale=qs, start=True, stop=True)

        def add_bias(r, g, n=1):
            biased[r, g] = held.tile([P, n * P], F32, name="biased%d%d" % (r, g))
            nc.scalar.activation(biased[r, g][:], banks[r, 2 * g][:], IDENTITY, bias=bias_even[:, g : g + 1])

        def take_larger(r, g, n=1):
            larger[r, g] = held.tile([P, n * P], F32, name="larger%d%d" % (r, g))
            nc.vector.scalar_tensor_tensor(larger[r, g][:], banks[r, 2 * g + 1][:], bias[:, 2 * g + 1 : 2 * g + 2], biased[r, g][:], ADD, MAX)

        gather(3, 0, HALF)
        gather(3, HALF, N)
        join(nc.scalar.copy, U32, 0, 1)
        join(nc.vector.tensor_copy, I32, 1, 1)
        join(nc.vector.tensor_copy, I32, 2, 2)
        nc.scalar.copy(woven_first[:].rearrange("p (c i t) -> p c t i", i=4, t=PACK), q_dealt[:, 0])
        weave(nc.scalar.copy, P, P)
        quantise(0, 2)
        quantise(2, 1)
        nc.vector.quantize_mx(out=codes[:, span(5, 1)].bitcast(FP8X4), scales=scales[:, span(5, 1)], in_=woven_first[:])
        last_codes = held.tile([P, CHUNK], U32, name="last_codes", tag="first_rows_then_codes", align_bytes=64)
        nc.vector.quantize_mx(out=last_codes[:].bitcast(FP8X4), scales=scales[:, span(3, 1)], in_=woven[:, 3 * CHUNK * PACK : 4 * CHUNK * PACK])
        quantise(4, 1)
        def multiply_rows(r, g, bank):
            (q, qs), (k, ks) = operand("q", r, 1), operand("c", 2 * g, 2)
            banks[r, g, "rows"] = psum.tile([P, HALF], F32, name="bank%d" % bank)
            nc.tensor.matmul_mx(out=banks[r, g, "rows"][:], lhsT=q, lhsT_scale=qs, rhs=k, rhs_scale=ks, start=True, stop=True)

        def add_row(r, g):
            biased[r, g] = held.tile([P, HALF], F32, name="biased%d%d" % (r, g), tag="bias_then_sums" if g == 0 else "sums")
            nc.vector.tensor_tensor(biased[r, g][:], banks[r, g, "rows"][:], bias_row[:, g * HALF : (g + 1) * HALF], ADD)

        def largest(r, g):
            nc.vector.reduce_max(best[:, r, 8 * g : 8 * (g + 1)], biased[r, g][:].rearrange("p (u j i) -> p j u i", u=2, i=RUN), axis=mybir.AxisListType.XY)

        def finish(r, first, count, bank):
            turned = psum.tile([P, count, P], F32, name="bank%d" % bank)
            for g in range(count):
                nc.tensor.transpose(turned[:, g, :], larger[r, first + g][:], identity[:])
            nc.vector.reduce_max(best[:, r, 8 * first : 8 * (first + count)], turned[:].rearrange("p g (j i) -> p (g j) i", i=RUN), axis=mybir.AxisListType.X)

        for s in (0, 2, 1, 3):
            multiply(0, s)
        multiply_rows(1, 0, 4)
        banks[1, 1, "rows"] = psum.tile([P, HALF], F32, name="bank5")
        for s in range(2):
            (q, qs), (k, ks) = operand("q", 1, 1), operand("c", 2 + s, 1)
            nc.tensor.matmul_mx(out=banks[1, 1, "rows"][:, span(s, 1)], lhsT=q, lhsT_scale=qs, rhs=k, rhs_scale=ks, start=True, stop=True)
        add_bias(0, 0)
        add_bias(0, 1)
        take_larger(0, 0)
        take_larger(0, 1)
        add_row(1, 0)
        add_row(1, 1)
        largest(1, 0)
        largest(1, 1)
        finish(0, 0, 2, 0)
        nc.sync.dma_start(out[0].rearrange("(p r) j -> p (r j)", r=ROWS), best[:].rearrange("p r j -> p (r j)"))
